import numpy as np
import ml_dtypes


def mxq(x, axis, fmt="e4m3"):
    dtype, down = {"e4m3": (ml_dtypes.float8_e4m3fn, 7), "e5m2": (ml_dtypes.float8_e5m2, 14)}[fmt]
    v = np.moveaxis(np.asarray(x, np.float32).astype(ml_dtypes.bfloat16).astype(np.float64), axis, -1)
    blocks = v.reshape(v.shape[:-1] + (-1, 32))
    amax = np.abs(blocks).max(-1, keepdims=True)
    byte = np.maximum(np.where(amax > 0, np.frexp(amax)[1] - 1 + 127, 0) - down, 1)
    scale = np.exp2(byte - 127.0)
    codes = (blocks / scale).astype(np.float32).astype(dtype).astype(np.float64)
    return np.moveaxis((codes * scale).reshape(v.shape), -1, axis)


WIDE = False


def mx_kscale(k):
    if not WIDE:
        return np.ones(k)
    levels = np.array([10, -10, 5, -5, 0])
    if k % 512:
        return np.exp2(np.random.permutation(np.resize(levels, k // 32))).repeat(32)
    a = np.empty((k // 512, 16))
    for p in range(k // 512):
        a[p, :8] = np.random.permutation(np.resize(levels, 8))
        for g in range(8):
            far = levels[np.abs(levels - a[p, g]) >= 10]
            a[p, g + 8] = far[np.random.randint(len(far))]
    return np.exp2(a.ravel()).repeat(32)


def f64(x):
    return np.asarray(x).astype(np.float64)


def striped(idx):
    return np.tile(idx.reshape(-1, 16).T, (8, 1)).astype(np.uint16)


def unstriped(offs):
    return offs[:16].T.reshape(-1).astype(np.int64)


def striped8(idx):
    return np.concatenate([x.reshape(-1, 16).T for x in idx]).astype(np.uint16)


def runs(offs, k):
    lists = np.stack([offs[16 * r : 16 * r + 16].T.reshape(-1) for r in range(8)]).astype(np.int64)
    return lists[np.arange(k) % 512 // 64]


def pack_weight(w):
    k, n = w.shape
    w = f64(np.asarray(w, np.float32).astype(ml_dtypes.bfloat16)).reshape(k // 32, 32, n)
    amax = np.abs(w).max(1)
    byte = np.clip(np.where(amax > 0, np.frexp(amax)[1] - 1 + 127 - 7, 1), 1, 254)
    scaled = (w * np.exp2(127.0 - byte)[:, None, :]).reshape(k, n).astype(np.float32)
    words = np.ascontiguousarray(scaled.reshape(k // 512, 128, 4, n).transpose(0, 1, 3, 2)).astype(ml_dtypes.float8_e4m3fn).view(np.uint8)
    return words, np.ascontiguousarray(byte.astype(np.uint8).reshape(k // 512, 16, n))


def unpack_weight(words, scales):
    g, p, n, _ = words.shape
    vals = np.ascontiguousarray(words).view(ml_dtypes.float8_e4m3fn).astype(np.float64) * np.repeat(np.exp2(scales.astype(np.float64) - 127.0), 8, axis=1)[..., None]
    return vals.transpose(0, 1, 3, 2).reshape(g * 512, n)


def relu(v):
    return np.maximum(v, 0.0)


K, T, S, N, U, H = 512, 2048, 512, 512, 1024, 512


def setup_inputs():
    n = np.random.standard_normal
    s = mx_kscale(K)[:, None]
    u = mx_kscale(S)
    packed_xT = pack_weight(n((K, T)) * s)
    return {
        "x_words": packed_xT[0],
        "x_scales": packed_xT[1],
        "wa": (n((K, H)) / np.sqrt(K) / s).astype(np.float32),
        "gt": (np.random.uniform(0.5, 1.5, (S, 1)) * u[:, None]).astype(np.float32),
        "w1": (n((S, N)) / np.sqrt(S) / u[:, None]).astype(np.float32),
        "offs": striped(np.random.permutation(T)[:S]),
        "fl": striped8(np.stack([np.random.permutation(U)[:H] for _ in range(8)])),
    }


def reference(x_words, x_scales, wa, gt, w1, offs, fl):
    xq = unpack_weight(x_words, x_scales)[:, unstriped(offs)]
    y = xq.T @ mxq(f64(wa), 0, "e4m3")
    e = f64(gt) * relu(y)
    z = np.zeros((S, U))
    z[np.arange(S)[:, None], runs(fl, S)] = e
    return mxq(f64(w1), 0, "e4m3").T @ mxq(z, 0, "e4m3")

@@ -1,0 +1,181 @@
+from contextlib import ExitStack
+
+import concourse.mybir as mybir
+
+K, T, S, N, U, H = 512, 2048, 512, 512, 1024, 512
+FLOPS = 2 * K * S * H + 2 * S * N * U
+
+F32 = mybir.dt.float32
+BF16 = mybir.dt.bfloat16
+I32 = mybir.dt.int32
+U32 = mybir.dt.uint32
+U16 = mybir.dt.uint16
+U8 = mybir.dt.uint8
+FP8X4 = mybir.dt.float8_e4m3fn_x4
+RELU = mybir.ActivationFunctionType.Relu
+COPY = mybir.ActivationFunctionType.Copy
+MULT = mybir.AluOpType.mult
+
+P = 128
+PACK = 4
+HALF = H // 2
+CHUNK = 256
+LIST_ROWS = 16
+
+
+def interleave(copy, grouped, raw):
+    copy(
+        out=grouped.rearrange("p (c i) t -> p c t i", i=4),
+        in_=raw.rearrange("p t (c i) -> p c t i", i=4),
+    )
+
+
+def tile_picked_blkmix_relu_p_kernel(
+    tc, x_words, x_scales, wa, gt, w1, offs, fl, out
+):
+    nc = tc.nc
+    with ExitStack() as ctx:
+        keep = ctx.enter_context(tc.tile_pool(name="keep", bufs=1))
+        psum = ctx.enter_context(tc.psum_pool(name="psum", bufs=8))
+
+        picks = keep.tile([P, S // LIST_ROWS], U16, name="picks")
+        places = keep.tile([P, H // LIST_ROWS], U16, name="places")
+        table_words = keep.tile([P, T], I32, name="table_words", align_bytes=64)
+        table_scales = keep.tile([P, T], U8, name="table_scales", align_bytes=64)
+        gate = keep.tile([P, PACK], F32, name="gate")
+        wa_rows = wa.rearrange("(p j) h -> p j h", j=PACK)
+        wa_raw = [keep.tile([P, PACK, HALF], F32, name="wa_raw%d" % h) for h in range(2)]
+        w1_raw = keep.tile([P, PACK, N], F32, name="w1_raw")
+
+        nc.vector.memset(table_scales[:].bitcast(I32), 0)
+
+        nc.sync.dma_start(picks[:], offs)
+        nc.sync.dma_start(wa_raw[0][:], wa_rows[:, :, 0:HALF])
+        nc.sync.dma_start(table_words[:], x_words[0].rearrange("p n t -> p (n t)").bitcast(I32))
+        nc.scalar.dma_start(gate[:], gt.rearrange("(p t) o -> p (t o)", t=PACK))
+        for q in range(4):
+            nc.scalar.dma_start(
+                table_scales[32 * q : 32 * q + 4, :].bitcast(I32),
+                x_scales[0, 4 * q : 4 * q + 4, :].bitcast(I32),
+            )
+        nc.sync.dma_start(wa_raw[1][:], wa_rows[:, :, HALF:H])
+        nc.sync.dma_start(places[:], fl)
+        nc.sync.dma_start(w1_raw[:], w1.rearrange("(p j) m -> p j m", j=PACK))
+
+        z = [keep.tile([P, U], F32, name="z%d" % t) for t in range(PACK)]
+        for t in range(PACK):
+            nc.vector.memset(z[t][:], 0.0)
+
+        wa_grouped = [keep.tile([P, HALF, PACK], BF16, name="wa_grouped%d" % h, align_bytes=64) for h in range(2)]
+        wa_codes = keep.tile([P, H], U32, name="wa_codes", align_bytes=64)
+        wa_scales = keep.tile([P, H], U8, name="wa_scales", align_bytes=64)
+
+        def quantize(codes, scales, grouped):
+            nc.vector.quantize_mx(
+                out=codes.bitcast(FP8X4), scales=scales, in_=grouped.rearrange("p w j -> p (w j)")
+            )
+
+        gate_wide = [keep.tile([P, H], F32, name="gate_wide%d" % t) for t in range(PACK)]
+        nc.scalar.activation(out=gate_wide[0][:], in_=gate[:, 0:1].to_broadcast([P, H]), func=COPY)
+        interleave(nc.scalar.copy, wa_grouped[0][:], wa_raw[0][:])
+        for t in range(1, PACK):
+            nc.scalar.copy(out=gate_wide[t][:], in_=gate[:, t : t + 1].to_broadcast([P, H]))
+
+        picked_scales = keep.tile([P, S], U8, name="picked_scales", align_bytes=64)
+        x_scale_plane = keep.tile([P, S], U8, name="x_scale_plane", align_bytes=64)
+        x_codes = keep.tile([P, S], U32, name="x_codes", align_bytes=64)
+        nc.vector.tensor_copy(picked_scales[:], table_scales[:].indirect(picks[:]))
+        quantize(wa_codes[:, 0:HALF], wa_scales[:, 0:HALF], wa_grouped[0][:])
+        nc.vector.tensor_copy(
+            x_scale_plane[:].rearrange("p (t m) -> p m t", t=PACK),
+            picked_scales[:].rearrange("p (m t) -> p m t", t=PACK),
+        )
+        nc.vector.tensor_copy(
+            x_codes[:].rearrange("p (t m) -> p m t", t=PACK),
+            table_words[:].bitcast(U32).indirect(picks[:]),
+        )
+
+        active = [keep.tile([P, H], F32, name="active%d" % t) for t in range(PACK)]
+
+        def project(t, h0, h1):
+            acc = psum.tile([P, 512], F32, name="acc")
+            nc.tensor.matmul_mx(
+                out=acc[:, 0 : h1 - h0],
+                lhsT=x_codes[:, t * P : (t + 1) * P].bitcast(FP8X4),
+                lhsT_scale=x_scale_plane[:, t * P : (t + 1) * P],
+                rhs=wa_codes[:, h0:h1].bitcast(FP8X4),
+                rhs_scale=wa_scales[:, h0:h1],
+                start=True,
+                stop=True,
+            )
+            nc.scalar.activation(out=active[t][:, h0:h1], in_=acc[:, 0 : h1 - h0], func=RELU)
+
+        def scatter(t, h0, h1):
+            nc.vector.tensor_tensor(
+                z[t][:].indirect(places[:, h0 // LIST_ROWS : h1 // LIST_ROWS]),
+                active[t][:, h0:h1],
+                gate_wide[t][:, h0:h1],
+                MULT,
+            )
+
+        chunks = U // CHUNK
+        z_grouped = [keep.tile([P, CHUNK, PACK], BF16, name="z_grouped%d" % c, align_bytes=64) for c in range(chunks)]
+
+        def round_plane(copy, t, c):
+            copy(out=z_grouped[c][:, :, t], in_=z[t][:, c * CHUNK : (c + 1) * CHUNK])
+
+        project(0, 0, HALF)
+        project(1, 0, HALF)
+        interleave(nc.scalar.copy, wa_grouped[1][:], wa_raw[1][:])
+        scatter(0, 0, HALF)
+        quantize(wa_codes[:, HALF:H], wa_scales[:, HALF:H], wa_grouped[1][:])
+        scatter(1, 0, HALF)
+        project(0, HALF, H)
+        project(1, HALF, H)
+        project(2, 0, H)
+        project(3, 0, H)
+
+        w1_grouped = keep.tile([P, N, PACK], BF16, name="w1_grouped", align_bytes=64)
+        w1_codes = keep.tile([P, N], U32, name="w1_codes", align_bytes=64)
+        w1_scales = keep.tile([P, N], U8, name="w1_scales", align_bytes=64)
+        interleave(nc.scalar.copy, w1_grouped[:], w1_raw[:])
+
+        scatter(0, HALF, H)
+        scatter(1, HALF, H)
+        for c in range(chunks):
+            round_plane(nc.scalar.copy, 0, c)
+        scatter(2, 0, H)
+        for c in range(chunks):
+            round_plane(nc.scalar.copy, 1, c)
+        quantize(w1_codes[:], w1_scales[:], w1_grouped[:])
+        scatter(3, 0, H)
+        for c in range(chunks):
+            nc.scalar.copy(
+                out=z_grouped[c][:, :, 2:4],
+                in_=z[2][:, c * CHUNK : (c + 1) * CHUNK].unsqueeze(2).to_broadcast([P, CHUNK, 2]),
+            )
+
+        out_rows = out.rearrange("(mt p) w -> p mt w", p=P)
+        for c in range(chunks):
+            z_codes = keep.tile([P, CHUNK], U32, name="z_codes%d" % c, align_bytes=64)
+            z_scales = keep.tile([P, CHUNK], U8, name="z_scales%d" % c, align_bytes=64)
+            round_plane(nc.vector.tensor_copy, 3, c)
+            quantize(z_codes[:], z_scales[:], z_grouped[c][:])
+            for pair in range(2):
+                acc = psum.tile([P, 512], F32, name="acc")
+                for i in range(2):
+                    mt = 2 * pair + i
+                    nc.tensor.matmul_mx(
+                        out=acc[:, i * CHUNK : (i + 1) * CHUNK],
+                        lhsT=w1_codes[:, mt * P : (mt + 1) * P].bitcast(FP8X4),
+                        lhsT_scale=w1_scales[:, mt * P : (mt + 1) * P],
+                        rhs=z_codes[:].bitcast(FP8X4),
+                        rhs_scale=z_scales[:],
+                        start=True,
+                        stop=True,
+                    )
+                result = keep.tile([P, 2, CHUNK], F32, name="result%d_%d" % (c, pair))
+                nc.scalar.copy(out=result[:].rearrange("p a w -> p (a w)"), in_=acc[:])
+                nc.sync.dma_start(
+                    out_rows[:, 2 * pair : 2 * pair + 2, c * CHUNK : (c + 1) * CHUNK], result[:]
+                )

@@ -18,9 +18,12 @@ MULT = mybir.AluOpType.mult
 
 P = 128
 PACK = 4
+RUN = 8
+BLOCKS = S // (PACK * RUN)
 HALF = H // 2
 CHUNK = 256
 LIST_ROWS = 16
+BANK = 512
 
 
 def interleave(copy, grouped, raw):
@@ -36,35 +39,43 @@ def tile_picked_blkmix_relu_p_kernel(
     nc = tc.nc
     with ExitStack() as ctx:
         keep = ctx.enter_context(tc.tile_pool(name="keep", bufs=1))
+        shared = ctx.enter_context(tc.tile_pool(name="shared", bufs=1))
+        planes = ctx.enter_context(tc.tile_pool(name="planes", bufs=1))
         psum = ctx.enter_context(tc.psum_pool(name="psum", bufs=8))
 
         picks = keep.tile([P, S // LIST_ROWS], U16, name="picks")
         places = keep.tile([P, H // LIST_ROWS], U16, name="places")
         table_words = keep.tile([P, T], I32, name="table_words", align_bytes=64)
         table_scales = keep.tile([P, T], U8, name="table_scales", align_bytes=64)
-        gate = keep.tile([P, PACK], F32, name="gate")
+        gate = [keep.tile([P, 1], F32, name="gate%d" % t) for t in range(PACK)]
         wa_rows = wa.rearrange("(p j) h -> p j h", j=PACK)
-        wa_raw = [keep.tile([P, PACK, HALF], F32, name="wa_raw%d" % h) for h in range(2)]
-        w1_raw = keep.tile([P, PACK, N], F32, name="w1_raw")
+        wa_raw = [keep.tile([P, PACK, HALF], F32, name="wa_raw%d" % h, tag="stage%d" % h) for h in range(2)]
+        w1_raw = shared.tile([P, PACK, N], F32, name="w1_raw", offset=0)
 
         nc.vector.memset(table_scales[:].bitcast(I32), 0)
 
         nc.sync.dma_start(picks[:], offs)
         nc.sync.dma_start(wa_raw[0][:], wa_rows[:, :, 0:HALF])
-        nc.sync.dma_start(table_words[:], x_words[0].rearrange("p n t -> p (n t)").bitcast(I32))
-        nc.scalar.dma_start(gate[:], gt.rearrange("(p t) o -> p (t o)", t=PACK))
         for q in range(4):
-            nc.scalar.dma_start(
+            nc.sync.dma_start(
                 table_scales[32 * q : 32 * q + 4, :].bitcast(I32),
                 x_scales[0, 4 * q : 4 * q + 4, :].bitcast(I32),
             )
+        nc.sync.dma_start(table_words[:], x_words[0].rearrange("p n t -> p (n t)").bitcast(I32))
         nc.sync.dma_start(wa_raw[1][:], wa_rows[:, :, HALF:H])
         nc.sync.dma_start(places[:], fl)
-        nc.sync.dma_start(w1_raw[:], w1.rearrange("(p j) m -> p j m", j=PACK))
-
-        z = [keep.tile([P, U], F32, name="z%d" % t) for t in range(PACK)]
+        w1_rows = w1.rearrange("(b t q) m -> t b q m", t=PACK, q=RUN)
         for t in range(PACK):
+            nc.sync.dma_start(w1_raw[:, t, :], w1_rows[t])
+        gt_rows = gt.rearrange("(b t q) o -> t b q o", t=PACK, q=RUN)
+        for t in range(PACK):
+            nc.sync.dma_start(gate[t][:], gt_rows[t])
+
+        z = [planes.tile([P, U], F32, name="z%d" % t, offset=t * U * 4) for t in range(PACK)]
+        for t in range(2):
             nc.vector.memset(z[t][:], 0.0)
+        for t in range(2, PACK):
+            nc.scalar.activation(out=z[t][:], in_=z[t - 2][:], func=COPY)
 
         wa_grouped = [keep.tile([P, HALF, PACK], BF16, name="wa_grouped%d" % h, align_bytes=64) for h in range(2)]
         wa_codes = keep.tile([P, H], U32, name="wa_codes", align_bytes=64)
@@ -75,11 +86,7 @@ def tile_picked_blkmix_relu_p_kernel(
                 out=codes.bitcast(FP8X4), scales=scales, in_=grouped.rearrange("p w j -> p (w j)")
             )
 
-        gate_wide = [keep.tile([P, H], F32, name="gate_wide%d" % t) for t in range(PACK)]
-        nc.scalar.activation(out=gate_wide[0][:], in_=gate[:, 0:1].to_broadcast([P, H]), func=COPY)
         interleave(nc.scalar.copy, wa_grouped[0][:], wa_raw[0][:])
-        for t in range(1, PACK):
-            nc.scalar.copy(out=gate_wide[t][:], in_=gate[:, t : t + 1].to_broadcast([P, H]))
 
         picked_scales = keep.tile([P, S], U8, name="picked_scales", align_bytes=64)
         x_scale_plane = keep.tile([P, S], U8, name="x_scale_plane", align_bytes=64)
@@ -87,18 +94,20 @@ def tile_picked_blkmix_relu_p_kernel(
         nc.vector.tensor_copy(picked_scales[:], table_scales[:].indirect(picks[:]))
         quantize(wa_codes[:, 0:HALF], wa_scales[:, 0:HALF], wa_grouped[0][:])
         nc.vector.tensor_copy(
-            x_scale_plane[:].rearrange("p (t m) -> p m t", t=PACK),
-            picked_scales[:].rearrange("p (m t) -> p m t", t=PACK),
+            x_scale_plane[:].bitcast(I32).rearrange("p (t b w) -> p t b w", t=PACK, b=BLOCKS),
+            picked_scales[:].bitcast(I32).rearrange("p (b t w) -> p t b w", t=PACK, b=BLOCKS),
         )
         nc.vector.tensor_copy(
-            x_codes[:].rearrange("p (t m) -> p m t", t=PACK),
+            x_codes[:].rearrange("p (t b q) -> p b t q", t=PACK, q=RUN),
             table_words[:].bitcast(U32).indirect(picks[:]),
         )
+        interleave(nc.vector.tensor_copy, wa_grouped[1][:], wa_raw[1][:])
+        quantize(wa_codes[:, HALF:H], wa_scales[:, HALF:H], wa_grouped[1][:])
 
-        active = [keep.tile([P, H], F32, name="active%d" % t) for t in range(PACK)]
+        active = [keep.tile([P, H], F32, name="active%d" % t, tag="stage%d" % (t + 1)) for t in range(PACK)]
 
         def project(t, h0, h1):
-            acc = psum.tile([P, 512], F32, name="acc")
+            acc = psum.tile([P, BANK], F32, name="acc")
             nc.tensor.matmul_mx(
                 out=acc[:, 0 : h1 - h0],
                 lhsT=x_codes[:, t * P : (t + 1) * P].bitcast(FP8X4),
@@ -111,62 +120,71 @@ def tile_picked_blkmix_relu_p_kernel(
             nc.scalar.activation(out=active[t][:, h0:h1], in_=acc[:, 0 : h1 - h0], func=RELU)
 
         def scatter(t, h0, h1):
-            nc.vector.tensor_tensor(
+            nc.vector.tensor_copy(
                 z[t][:].indirect(places[:, h0 // LIST_ROWS : h1 // LIST_ROWS]),
                 active[t][:, h0:h1],
-                gate_wide[t][:, h0:h1],
-                MULT,
             )
 
         chunks = U // CHUNK
-        z_grouped = [keep.tile([P, CHUNK, PACK], BF16, name="z_grouped%d" % c, align_bytes=64) for c in range(chunks)]
+        WIDE = U // 2
+        z_grouped = [
+            shared.tile([P, WIDE, PACK], BF16, name="z_grouped%d" % c, align_bytes=64, offset=c * WIDE * PACK * 2)
+            for c in range(2)
+        ]
 
-        def round_plane(copy, t, c):
-            copy(out=z_grouped[c][:, :, t], in_=z[t][:, c * CHUNK : (c + 1) * CHUNK])
+        def round_plane(t, c):
+            nc.scalar.activation(
+                out=z_grouped[c][:, :, t], in_=z[t][:, c * WIDE : (c + 1) * WIDE], func=COPY, scale=gate[t][:]
+            )
 
         project(0, 0, HALF)
-        project(1, 0, HALF)
-        interleave(nc.scalar.copy, wa_grouped[1][:], wa_raw[1][:])
-        scatter(0, 0, HALF)
-        quantize(wa_codes[:, HALF:H], wa_scales[:, HALF:H], wa_grouped[1][:])
-        scatter(1, 0, HALF)
         project(0, HALF, H)
-        project(1, HALF, H)
-        project(2, 0, H)
-        project(3, 0, H)
+        for t in range(1, PACK):
+            project(t, 0, H)
 
         w1_grouped = keep.tile([P, N, PACK], BF16, name="w1_grouped", align_bytes=64)
         w1_codes = keep.tile([P, N], U32, name="w1_codes", align_bytes=64)
         w1_scales = keep.tile([P, N], U8, name="w1_scales", align_bytes=64)
         interleave(nc.scalar.copy, w1_grouped[:], w1_raw[:])
 
+        scatter(0, 0, HALF)
         scatter(0, HALF, H)
-        scatter(1, HALF, H)
-        for c in range(chunks):
-            round_plane(nc.scalar.copy, 0, c)
+
+        scatter(1, 0, H)
+        for c in range(2):
+            round_plane(0, c)
         scatter(2, 0, H)
-        for c in range(chunks):
-            round_plane(nc.scalar.copy, 1, c)
+        for c in range(2):
+            round_plane(1, c)
         quantize(w1_codes[:], w1_scales[:], w1_grouped[:])
         scatter(3, 0, H)
-        for c in range(chunks):
-            nc.scalar.copy(
+        for c in range(2):
+            nc.scalar.activation(
                 out=z_grouped[c][:, :, 2:4],
-                in_=z[2][:, c * CHUNK : (c + 1) * CHUNK].unsqueeze(2).to_broadcast([P, CHUNK, 2]),
+                in_=z[2][:, c * WIDE : (c + 1) * WIDE].unsqueeze(2).to_broadcast([P, WIDE, 2]),
+                func=COPY,
+                scale=gate[2][:],
             )
 
         out_rows = out.rearrange("(mt p) w -> p mt w", p=P)
-        for c in range(chunks):
-            z_codes = keep.tile([P, CHUNK], U32, name="z_codes%d" % c, align_bytes=64)
-            z_scales = keep.tile([P, CHUNK], U8, name="z_scales%d" % c, align_bytes=64)
-            round_plane(nc.vector.tensor_copy, 3, c)
-            quantize(z_codes[:], z_scales[:], z_grouped[c][:])
-            for pair in range(2):
-                acc = psum.tile([P, 512], F32, name="acc")
-                for i in range(2):
-                    mt = 2 * pair + i
+        result_planes = (2, 2, 0, 0, 1, 1, 3, 3)
+        stored = 0
+        first = 0
+        for c, width in enumerate((128, 128, 256, 256, 256)):
+            cols = slice(first, first + width)
+            part = z_grouped[first // WIDE][:, first % WIDE : first % WIDE + width, :]
+            first = first + width
+            z_codes = keep.tile([P, width], U32, name="z_codes%d" % c, align_bytes=64)
+            z_scales = keep.tile([P, width], U8, name="z_scales%d" % c, align_bytes=64)
+            nc.vector.tensor_scalar(part[:, :, 3], z[3][:, cols], gate[3][:], None, MULT)
+            quantize(z_codes[:], z_scales[:], part)
+            per_bank = BANK // width
+            for mt0 in range(0, N // P, per_bank):
+                acc = psum.tile([P, BANK], F32, name="acc")
+                for i in range(per_bank):
+                    mt = mt0 + i
                     nc.tensor.matmul_mx(
-                        out=acc[:, i * CHUNK : (i + 1) * CHUNK],
+                        out=acc[:, i * width : (i + 1) * width],
                         lhsT=w1_codes[:, mt * P : (mt + 1) * P].bitcast(FP8X4),
                         lhsT_scale=w1_scales[:, mt * P : (mt + 1) * P],
                         rhs=z_codes[:].bitcast(FP8X4),
@@ -174,8 +192,12 @@ def tile_picked_blkmix_relu_p_kernel(
                         start=True,
                         stop=True,
                     )
-                result = keep.tile([P, 2, CHUNK], F32, name="result%d_%d" % (c, pair))
-                nc.scalar.copy(out=result[:].rearrange("p a w -> p (a w)"), in_=acc[:])
-                nc.sync.dma_start(
-                    out_rows[:, 2 * pair : 2 * pair + 2, c * CHUNK : (c + 1) * CHUNK], result[:]
+                result = planes.tile(
+                    [P, per_bank, width],
+                    F32,
+                    name="result%d" % stored,
+                    offset=(result_planes[stored] * U + stored % 2 * BANK) * 4,
                 )
+                stored = stored + 1
+                nc.scalar.copy(out=result[:].rearrange("p a w -> p (a w)"), in_=acc[:])
+                nc.sync.dma_start(out_rows[:, mt0 : mt0 + per_bank, cols], result[:])

@@ -45,17 +45,17 @@ def tile_picked_blkmix_relu_p_kernel(
 
         picks = keep.tile([P, S // LIST_ROWS], U16, name="picks")
         places = keep.tile([P, H // LIST_ROWS], U16, name="places")
-        table_words = keep.tile([P, T], I32, name="table_words", align_bytes=64)
+        table_words = keep.tile([P, T], I32, name="table_words", align_bytes=256)
         table_scales = keep.tile([P, T], U8, name="table_scales", align_bytes=64)
         gate = [keep.tile([P, 1], F32, name="gate%d" % t) for t in range(PACK)]
         wa_rows = wa.rearrange("(p j) h -> p j h", j=PACK)
-        wa_raw = [keep.tile([P, PACK, HALF], F32, name="wa_raw%d" % h, tag="stage%d" % h) for h in range(2)]
-        w1_raw = shared.tile([P, PACK, N], F32, name="w1_raw", offset=0)
+        wa_raw = [keep.tile([P, PACK, HALF], F32, name="wa_raw%d" % h, tag="stage%d" % h, align_bytes=256) for h in range(2)]
+        w1_raw = shared.tile([P, PACK, N], F32, name="w1_raw", align_bytes=256, offset=2048)
 
         nc.vector.memset(table_scales[:].bitcast(I32), 0)
 
-        nc.sync.dma_start(picks[:], offs)
         nc.sync.dma_start(wa_raw[0][:], wa_rows[:, :, 0:HALF])
+        nc.sync.dma_start(picks[:], offs)
         for q in range(4):
             nc.sync.dma_start(
                 table_scales[32 * q : 32 * q + 4, :].bitcast(I32),
@@ -104,7 +104,7 @@ def tile_picked_blkmix_relu_p_kernel(
         interleave(nc.vector.tensor_copy, wa_grouped[1][:], wa_raw[1][:])
         quantize(wa_codes[:, HALF:H], wa_scales[:, HALF:H], wa_grouped[1][:])
 
-        active = [keep.tile([P, H], F32, name="active%d" % t, tag="stage%d" % (t + 1)) for t in range(PACK)]
+        active = [keep.tile([P, H], F32, name="active%d" % t, tag="stage%d" % (t + 1), align_bytes=256) for t in range(PACK)]
 
         def project(t, h0, h1):
             acc = psum.tile([P, BANK], F32, name="acc")
@@ -125,17 +125,21 @@ def tile_picked_blkmix_relu_p_kernel(
                 active[t][:, h0:h1],
             )
 
-        chunks = U // CHUNK
-        WIDE = U // 2
+        parts = ((0, 256), (256, 256), (512, 512))
         z_grouped = [
-            shared.tile([P, WIDE, PACK], BF16, name="z_grouped%d" % c, align_bytes=64, offset=c * WIDE * PACK * 2)
-            for c in range(2)
+            shared.tile([P, width, PACK], BF16, name="z_grouped%d" % c, align_bytes=64, offset=place)
+            for c, ((first, width), place) in enumerate(zip(parts, (1024, 3072, 9216)))
+        ]
+        staged = [
+            shared.tile([P, 2, width], BF16, name="staged%d" % c, offset=5120 + 4 * first)
+            for c, (first, width) in enumerate(parts)
         ]
 
-        def round_plane(t, c):
-            nc.scalar.activation(
-                out=z_grouped[c][:, :, t], in_=z[t][:, c * WIDE : (c + 1) * WIDE], func=COPY, scale=gate[t][:]
-            )
+        def stage_plane(t):
+            for c, (first, width) in enumerate(parts):
+                nc.scalar.activation(
+                    out=staged[c][:, t, :], in_=z[t][:, first : first + width], func=COPY, scale=gate[t][:]
+                )
 
         project(0, 0, HALF)
         project(0, HALF, H)
@@ -151,34 +155,37 @@ def tile_picked_blkmix_relu_p_kernel(
         scatter(0, HALF, H)
 
         scatter(1, 0, H)
-        for c in range(2):
-            round_plane(0, c)
+        stage_plane(0)
         scatter(2, 0, H)
-        for c in range(2):
-            round_plane(1, c)
+        stage_plane(1)
+        for c in range(len(parts)):
+            nc.scalar.copy(
+                out=z_grouped[c][:, :, 0:2],
+                in_=staged[c][:].rearrange("p t w -> p w t"),
+            )
         quantize(w1_codes[:], w1_scales[:], w1_grouped[:])
         scatter(3, 0, H)
-        for c in range(2):
+        for c, (first, width) in enumerate(parts):
             nc.scalar.activation(
                 out=z_grouped[c][:, :, 2:4],
-                in_=z[2][:, c * WIDE : (c + 1) * WIDE].unsqueeze(2).to_broadcast([P, WIDE, 2]),
+                in_=z[2][:, first : first + width].unsqueeze(2).to_broadcast([P, width, 2]),
                 func=COPY,
                 scale=gate[2][:],
             )
 
         out_rows = out.rearrange("(mt p) w -> p mt w", p=P)
-        result_planes = (2, 2, 0, 0, 1, 1, 3, 3)
+        result_places = (8192, 9216, 10240, 0, 2048, 4096, 6144, 12288, 14336)
         stored = 0
-        first = 0
-        for c, width in enumerate((128, 128, 256, 256, 256)):
-            cols = slice(first, first + width)
-            part = z_grouped[first // WIDE][:, first % WIDE : first % WIDE + width, :]
-            first = first + width
+        late = []
+        for c, (k, start, width, per_bank) in enumerate(
+            ((0, 0, 128, 2), (0, 128, 128, 4), (1, 0, 256, 2), (2, 0, 256, 2), (2, 256, 256, 2))
+        ):
+            cols = slice(parts[k][0] + start, parts[k][0] + start + width)
+            part = z_grouped[k][:, start : start + width, :]
             z_codes = keep.tile([P, width], U32, name="z_codes%d" % c, align_bytes=64)
             z_scales = keep.tile([P, width], U8, name="z_scales%d" % c, align_bytes=64)
             nc.vector.tensor_scalar(part[:, :, 3], z[3][:, cols], gate[3][:], None, MULT)
             quantize(z_codes[:], z_scales[:], part)
-            per_bank = BANK // width
             for mt0 in range(0, N // P, per_bank):
                 acc = psum.tile([P, BANK], F32, name="acc")
                 for i in range(per_bank):
@@ -192,12 +199,21 @@ def tile_picked_blkmix_relu_p_kernel(
                         start=True,
                         stop=True,
                     )
+                if k == 2 and mt0 == 0:
+                    copy = nc.vector.tensor_copy
+                    result = shared.tile(
+                        [P, per_bank, width], F32, name="result%d" % stored, align_bytes=256, offset=9216 + 8 * start
+                    )
+                    late.append((result, acc, mt0, cols))
+                    stored = stored + 1
+                    continue
+                copy = nc.scalar.copy
                 result = planes.tile(
-                    [P, per_bank, width],
-                    F32,
-                    name="result%d" % stored,
-                    offset=(result_planes[stored] * U + stored % 2 * BANK) * 4,
+                    [P, per_bank, width], F32, name="result%d" % stored, align_bytes=256, offset=result_places[stored]
                 )
                 stored = stored + 1
-                nc.scalar.copy(out=result[:].rearrange("p a w -> p (a w)"), in_=acc[:])
+                copy(out=result[:].rearrange("p a w -> p (a w)"), in_=acc[:, 0 : per_bank * width])
                 nc.sync.dma_start(out_rows[:, mt0 : mt0 + per_bank, cols], result[:])
+        for result, acc, mt0, cols in late:
+            nc.vector.tensor_copy(out=result[:].rearrange("p a w -> p (a w)"), in_=acc[:])
+            nc.sync.dma_start(out_rows[:, mt0 : mt0 + 2, cols], result[:])

@@ -20,10 +20,11 @@ P = 128
 PACK = 4
 RUN = 8
 BLOCKS = S // (PACK * RUN)
-HALF = H // 2
-CHUNK = 256
 LIST_ROWS = 16
 BANK = 512
+WA_PIECES = ((0, 128), (128, 256), (256, 512))
+CHUNKS = ((0, 128), (128, 384), (384, 512), (512, 1024))
+STORES = ((0, 1, 2), (1, 2, 2), (2, 4, 1))
 
 
 def interleave(copy, grouped, raw):
@@ -40,7 +41,6 @@ def tile_picked_blkmix_relu_p_kernel(
     with ExitStack() as ctx:
         keep = ctx.enter_context(tc.tile_pool(name="keep", bufs=1))
         shared = ctx.enter_context(tc.tile_pool(name="shared", bufs=1))
-        planes = ctx.enter_context(tc.tile_pool(name="planes", bufs=1))
         psum = ctx.enter_context(tc.psum_pool(name="psum", bufs=8))
 
         picks = keep.tile([P, S // LIST_ROWS], U16, name="picks")
@@ -49,12 +49,19 @@ def tile_picked_blkmix_relu_p_kernel(
         table_scales = keep.tile([P, T], U8, name="table_scales", align_bytes=64)
         gate = [keep.tile([P, 1], F32, name="gate%d" % t) for t in range(PACK)]
         wa_rows = wa.rearrange("(p j) h -> p j h", j=PACK)
-        wa_raw = [keep.tile([P, PACK, HALF], F32, name="wa_raw%d" % h, tag="stage%d" % h, align_bytes=256) for h in range(2)]
-        w1_raw = shared.tile([P, PACK, N], F32, name="w1_raw", align_bytes=256, offset=2048)
+        wa_raw = [
+            shared.tile([P, PACK, h1 - h0], F32, name="wa_raw%d" % i, align_bytes=256, offset=16 * h0)
+            for i, (h0, h1) in enumerate(WA_PIECES)
+        ]
+        w1_raw = keep.tile([P, PACK, N], F32, name="w1_raw", align_bytes=256)
 
         nc.vector.memset(table_scales[:].bitcast(I32), 0)
 
-        nc.sync.dma_start(wa_raw[0][:], wa_rows[:, :, 0:HALF])
+        def load_wa(i):
+            h0, h1 = WA_PIECES[i]
+            nc.sync.dma_start(wa_raw[i][:], wa_rows[:, :, h0:h1])
+
+        load_wa(0)
         nc.sync.dma_start(picks[:], offs)
         for q in range(4):
             nc.sync.dma_start(
@@ -62,22 +69,26 @@ def tile_picked_blkmix_relu_p_kernel(
                 x_scales[0, 4 * q : 4 * q + 4, :].bitcast(I32),
             )
         nc.sync.dma_start(table_words[:], x_words[0].rearrange("p n t -> p (n t)").bitcast(I32))
-        nc.sync.dma_start(wa_raw[1][:], wa_rows[:, :, HALF:H])
+        load_wa(1)
         nc.sync.dma_start(places[:], fl)
+        load_wa(2)
+        gt_rows = gt.rearrange("(b t q) o -> t b q o", t=PACK, q=RUN)
         w1_rows = w1.rearrange("(b t q) m -> t b q m", t=PACK, q=RUN)
         for t in range(PACK):
             nc.sync.dma_start(w1_raw[:, t, :], w1_rows[t])
-        gt_rows = gt.rearrange("(b t q) o -> t b q o", t=PACK, q=RUN)
         for t in range(PACK):
             nc.sync.dma_start(gate[t][:], gt_rows[t])
 
-        z = [planes.tile([P, U], F32, name="z%d" % t, offset=t * U * 4) for t in range(PACK)]
-        for t in range(2):
+        z = [keep.tile([P, U if t % 2 else 2 * U], F32, name="z%d" % t, align_bytes=256) for t in range(PACK)]
+        for t in (1, 3):
             nc.vector.memset(z[t][:], 0.0)
-        for t in range(2, PACK):
-            nc.scalar.activation(out=z[t][:], in_=z[t - 2][:], func=COPY)
+        for t in (0, 2):
+            nc.scalar.activation(out=z[t][:, 0:U], in_=z[t + 1][:], func=COPY)
 
-        wa_grouped = [keep.tile([P, HALF, PACK], BF16, name="wa_grouped%d" % h, align_bytes=64) for h in range(2)]
+        wa_grouped = [
+            keep.tile([P, h1 - h0, PACK], BF16, name="wa_grouped%d" % i, tag="wa_grouped%d" % min(i, 1), align_bytes=64)
+            for i, (h0, h1) in enumerate(WA_PIECES)
+        ]
         wa_codes = keep.tile([P, H], U32, name="wa_codes", align_bytes=64)
         wa_scales = keep.tile([P, H], U8, name="wa_scales", align_bytes=64)
 
@@ -86,13 +97,16 @@ def tile_picked_blkmix_relu_p_kernel(
                 out=codes.bitcast(FP8X4), scales=scales, in_=grouped.rearrange("p w j -> p (w j)")
             )
 
-        interleave(nc.scalar.copy, wa_grouped[0][:], wa_raw[0][:])
+        def prepare_wa(i):
+            h0, h1 = WA_PIECES[i]
+            interleave(nc.scalar.copy, wa_grouped[i][:], wa_raw[i][:])
+            quantize(wa_codes[:, h0:h1], wa_scales[:, h0:h1], wa_grouped[i][:])
 
         picked_scales = keep.tile([P, S], U8, name="picked_scales", align_bytes=64)
         x_scale_plane = keep.tile([P, S], U8, name="x_scale_plane", align_bytes=64)
         x_codes = keep.tile([P, S], U32, name="x_codes", align_bytes=64)
         nc.vector.tensor_copy(picked_scales[:], table_scales[:].indirect(picks[:]))
-        quantize(wa_codes[:, 0:HALF], wa_scales[:, 0:HALF], wa_grouped[0][:])
+        prepare_wa(0)
         nc.vector.tensor_copy(
             x_scale_plane[:].bitcast(I32).rearrange("p (t b w) -> p t b w", t=PACK, b=BLOCKS),
             picked_scales[:].bitcast(I32).rearrange("p (b t w) -> p t b w", t=PACK, b=BLOCKS),
@@ -101,12 +115,8 @@ def tile_picked_blkmix_relu_p_kernel(
             x_codes[:].rearrange("p (t b q) -> p b t q", t=PACK, q=RUN),
             table_words[:].bitcast(U32).indirect(picks[:]),
         )
-        interleave(nc.vector.tensor_copy, wa_grouped[1][:], wa_raw[1][:])
-        quantize(wa_codes[:, HALF:H], wa_scales[:, HALF:H], wa_grouped[1][:])
 
-        active = [keep.tile([P, H], F32, name="active%d" % t, tag="stage%d" % (t + 1), align_bytes=256) for t in range(PACK)]
-
-        def project(t, h0, h1):
+        def project(t, h0, h1, place):
             acc = psum.tile([P, BANK], F32, name="acc")
             nc.tensor.matmul_mx(
                 out=acc[:, 0 : h1 - h0],
@@ -117,103 +127,90 @@ def tile_picked_blkmix_relu_p_kernel(
                 start=True,
                 stop=True,
             )
-            nc.scalar.activation(out=active[t][:, h0:h1], in_=acc[:, 0 : h1 - h0], func=RELU)
+            active = shared.tile([P, h1 - h0], F32, name="active%d_%d" % (t, h0), align_bytes=256, offset=place)
+            nc.scalar.activation(out=active[:], in_=acc[:, 0 : h1 - h0], func=RELU)
+            return active
 
-        def scatter(t, h0, h1):
-            nc.vector.tensor_copy(
-                z[t][:].indirect(places[:, h0 // LIST_ROWS : h1 // LIST_ROWS]),
-                active[t][:, h0:h1],
-            )
+        def scatter(t, h0, h1, values):
+            nc.vector.tensor_copy(z[t][:].indirect(places[:, h0 // LIST_ROWS : h1 // LIST_ROWS]), values[:])
 
-        parts = ((0, 256), (256, 256), (512, 512))
-        z_grouped = [
-            shared.tile([P, width, PACK], BF16, name="z_grouped%d" % c, align_bytes=64, offset=place)
-            for c, ((first, width), place) in enumerate(zip(parts, (1024, 3072, 9216)))
-        ]
-        staged = [
-            shared.tile([P, 2, width], BF16, name="staged%d" % c, offset=5120 + 4 * first)
-            for c, (first, width) in enumerate(parts)
-        ]
+        prepare_wa(1)
+        places_of = {(1, 0): 2048, (3, 0): 2560, (1, 1): 0, (3, 1): 4096, (1, 2): 8192, (3, 2): 9216}
+        for i, (h0, h1) in enumerate(WA_PIECES):
+            for t in (1, 3):
+                if (t, i) == (3, 1):
+                    prepare_wa(2)
+                scatter(t, h0, h1, project(t, h0, h1, places_of[(t, i)]))
 
-        def stage_plane(t):
-            for c, (first, width) in enumerate(parts):
-                nc.scalar.activation(
-                    out=staged[c][:, t, :], in_=z[t][:, first : first + width], func=COPY, scale=gate[t][:]
-                )
+        def weighted(t):
+            active = project(t, 0, H, 10240 + 1024 * t)
+            values = keep.tile([P, H], F32, name="values%d" % t, align_bytes=256)
+            nc.scalar.activation(out=values[:], in_=active[:], func=COPY, scale=gate[t][:])
+            return values
 
-        project(0, 0, HALF)
-        project(0, HALF, H)
-        for t in range(1, PACK):
-            project(t, 0, H)
+        def stage(t):
+            nc.scalar.activation(out=z[t - 1][:, U : 2 * U], in_=z[t][:], func=COPY, scale=gate[t][:])
+
+        values0 = weighted(0)
+        stage(1)
+        scatter(0, 0, H, values0)
+        values2 = weighted(2)
 
         w1_grouped = keep.tile([P, N, PACK], BF16, name="w1_grouped", align_bytes=64)
         w1_codes = keep.tile([P, N], U32, name="w1_codes", align_bytes=64)
         w1_scales = keep.tile([P, N], U8, name="w1_scales", align_bytes=64)
         interleave(nc.scalar.copy, w1_grouped[:], w1_raw[:])
-
-        scatter(0, 0, HALF)
-        scatter(0, HALF, H)
-
-        scatter(1, 0, H)
-        stage_plane(0)
-        scatter(2, 0, H)
-        stage_plane(1)
-        for c in range(len(parts)):
-            nc.scalar.copy(
-                out=z_grouped[c][:, :, 0:2],
-                in_=staged[c][:].rearrange("p t w -> p w t"),
-            )
         quantize(w1_codes[:], w1_scales[:], w1_grouped[:])
-        scatter(3, 0, H)
-        for c, (first, width) in enumerate(parts):
-            nc.scalar.activation(
-                out=z_grouped[c][:, :, 2:4],
-                in_=z[2][:, first : first + width].unsqueeze(2).to_broadcast([P, width, 2]),
-                func=COPY,
-                scale=gate[2][:],
+        stage(3)
+        scatter(2, 0, H, values2)
+
+        z_grouped = [
+            keep.tile([P, c1 - c0, PACK], BF16, name="z_grouped%d" % c, align_bytes=64)
+            for c, (c0, c1) in enumerate(CHUNKS)
+        ]
+
+        def write_pair(copy, t, c):
+            c0, c1 = CHUNKS[c]
+            copy(
+                out=z_grouped[c][:, :, t : t + 2],
+                in_=z[t][:].rearrange("p (r w) -> p w r", r=2)[:, c0:c1, :],
             )
+
+        for c in range(len(CHUNKS)):
+            write_pair(nc.scalar.copy, 0, c)
 
         out_rows = out.rearrange("(mt p) w -> p mt w", p=P)
-        result_places = (8192, 9216, 10240, 0, 2048, 4096, 6144, 12288, 14336)
-        stored = 0
-        late = []
-        for c, (k, start, width, per_bank) in enumerate(
-            ((0, 0, 128, 2), (0, 128, 128, 4), (1, 0, 256, 2), (2, 0, 256, 2), (2, 256, 256, 2))
-        ):
-            cols = slice(parts[k][0] + start, parts[k][0] + start + width)
-            part = z_grouped[k][:, start : start + width, :]
-            z_codes = keep.tile([P, width], U32, name="z_codes%d" % c, align_bytes=64)
-            z_scales = keep.tile([P, width], U8, name="z_scales%d" % c, align_bytes=64)
-            nc.vector.tensor_scalar(part[:, :, 3], z[3][:, cols], gate[3][:], None, MULT)
-            quantize(z_codes[:], z_scales[:], part)
-            for mt0 in range(0, N // P, per_bank):
-                acc = psum.tile([P, BANK], F32, name="acc")
-                for i in range(per_bank):
-                    mt = mt0 + i
-                    nc.tensor.matmul_mx(
-                        out=acc[:, i * width : (i + 1) * width],
-                        lhsT=w1_codes[:, mt * P : (mt + 1) * P].bitcast(FP8X4),
-                        lhsT_scale=w1_scales[:, mt * P : (mt + 1) * P],
-                        rhs=z_codes[:].bitcast(FP8X4),
-                        rhs_scale=z_scales[:],
-                        start=True,
-                        stop=True,
+        for first, last, tiles_a_store in STORES:
+            g0, g1 = CHUNKS[first][0], CHUNKS[last - 1][1]
+            result = keep.tile([P, N // P, g1 - g0], F32, name="result%d" % first, align_bytes=256)
+            for c in range(first, last):
+                c0, c1 = CHUNKS[c]
+                width = c1 - c0
+                z_codes = keep.tile([P, width], U32, name="z_codes%d" % c, align_bytes=64)
+                z_scales = keep.tile([P, width], U8, name="z_scales%d" % c, align_bytes=64)
+                write_pair(nc.vector.tensor_copy, 2, c)
+                quantize(z_codes[:], z_scales[:], z_grouped[c][:])
+                per_bank = 2 if c == 0 else BANK // width
+                for mt0 in range(0, N // P, per_bank):
+                    acc = psum.tile([P, BANK], F32, name="acc")
+                    for i in range(per_bank):
+                        mt = mt0 + i
+                        nc.tensor.matmul_mx(
+                            out=acc[:, i * width : (i + 1) * width],
+                            lhsT=w1_codes[:, mt * P : (mt + 1) * P].bitcast(FP8X4),
+                            lhsT_scale=w1_scales[:, mt * P : (mt + 1) * P],
+                            rhs=z_codes[:].bitcast(FP8X4),
+                            rhs_scale=z_scales[:],
+                            start=True,
+                            stop=True,
+                        )
+                    copy = nc.vector.tensor_copy if width == BANK and mt0 % 2 == 0 else nc.scalar.copy
+                    copy(
+                        out=result[:, mt0 : mt0 + per_bank, c0 - g0 : c1 - g0],
+                        in_=acc[:, 0 : per_bank * width].rearrange("p (a w) -> p a w", a=per_bank),
                     )
-                if k == 2 and mt0 == 0:
-                    copy = nc.vector.tensor_copy
-                    result = shared.tile(
-                        [P, per_bank, width], F32, name="result%d" % stored, align_bytes=256, offset=9216 + 8 * start
-                    )
-                    late.append((result, acc, mt0, cols))
-                    stored = stored + 1
-                    continue
-                copy = nc.scalar.copy
-                result = planes.tile(
-                    [P, per_bank, width], F32, name="result%d" % stored, align_bytes=256, offset=result_places[stored]
-                )
-                stored = stored + 1
-                copy(out=result[:].rearrange("p a w -> p (a w)"), in_=acc[:, 0 : per_bank * width])
-                nc.sync.dma_start(out_rows[:, mt0 : mt0 + per_bank, cols], result[:])
-        for result, acc, mt0, cols in late:
-            nc.vector.tensor_copy(out=result[:].rearrange("p a w -> p (a w)"), in_=acc[:])
-            nc.sync.dma_start(out_rows[:, mt0 : mt0 + 2, cols], result[:])
+                    if c == last - 1:
+                        for s0 in range(mt0, mt0 + per_bank, tiles_a_store):
+                            nc.sync.dma_start(
+                                out_rows[:, s0 : s0 + tiles_a_store, g0:g1], result[:, s0 : s0 + tiles_a_store, :]
+                            )

@@ -23,8 +23,10 @@ BLOCKS = S // (PACK * RUN)
 LIST_ROWS = 16
 BANK = 512
 WA_PIECES = ((0, 128), (128, 256), (256, 512))
-CHUNKS = ((0, 128), (128, 384), (384, 512), (512, 1024))
-STORES = ((0, 1, 2), (1, 2, 2), (2, 4, 1))
+PARTS = ((0, 256), (256, 512), (512, 768), (768, 1024))
+CHUNKS = ((0, 0, 128, 2), (0, 128, 256, 4), (1, 256, 512, 2), (2, 512, 768, 2), (3, 768, 1024, 2))
+ON_VECTOR = ((3, 0), (3, 2), (4, 2))
+LAST_CUT = 384
 
 
 def interleave(copy, grouped, raw):
@@ -135,82 +137,94 @@ def tile_picked_blkmix_relu_p_kernel(
             nc.vector.tensor_copy(z[t][:].indirect(places[:, h0 // LIST_ROWS : h1 // LIST_ROWS]), values[:])
 
         prepare_wa(1)
-        places_of = {(1, 0): 2048, (3, 0): 2560, (1, 1): 0, (3, 1): 4096, (1, 2): 8192, (3, 2): 9216}
+        places_of = {(1, 0): 2048, (3, 0): 2560, (1, 1): 4096, (3, 1): 4608, (1, 2): 8192, (3, 2): 9216}
         for i, (h0, h1) in enumerate(WA_PIECES):
             for t in (1, 3):
-                if (t, i) == (3, 1):
+                if (t, i) == (1, 1):
                     prepare_wa(2)
                 scatter(t, h0, h1, project(t, h0, h1, places_of[(t, i)]))
 
-        def weighted(t):
-            active = project(t, 0, H, 10240 + 1024 * t)
-            values = keep.tile([P, H], F32, name="values%d" % t, align_bytes=256)
-            nc.scalar.activation(out=values[:], in_=active[:], func=COPY, scale=gate[t][:])
+        def weigh(t, active, h0, h1):
+            values = keep.tile([P, h1 - h0], F32, name="values%d_%d" % (t, h0), align_bytes=256)
+            nc.scalar.activation(out=values[:], in_=active[:, h0:h1], func=COPY, scale=gate[t][:])
             return values
 
         def stage(t):
             nc.scalar.activation(out=z[t - 1][:, U : 2 * U], in_=z[t][:], func=COPY, scale=gate[t][:])
 
-        values0 = weighted(0)
-        stage(1)
-        scatter(0, 0, H, values0)
-        values2 = weighted(2)
-
-        w1_grouped = keep.tile([P, N, PACK], BF16, name="w1_grouped", align_bytes=64)
-        w1_codes = keep.tile([P, N], U32, name="w1_codes", align_bytes=64)
+        w1_grouped = [keep.tile([P, N // 2, PACK], BF16, name="w1_grouped%d" % h, align_bytes=64) for h in range(2)]
         w1_scales = keep.tile([P, N], U8, name="w1_scales", align_bytes=64)
-        interleave(nc.scalar.copy, w1_grouped[:], w1_raw[:])
-        quantize(w1_codes[:], w1_scales[:], w1_grouped[:])
-        stage(3)
-        scatter(2, 0, H, values2)
+
+        def round_w1(h):
+            interleave(nc.scalar.copy, w1_grouped[h][:], w1_raw[:, :, h * N // 2 : (h + 1) * N // 2])
+
+        def quantize_w1(h, tag):
+            codes = keep.tile([P, N // 2], U32, name="w1_codes%d" % h, tag=tag, align_bytes=256)
+            quantize(codes[:], w1_scales[:, h * N // 2 : (h + 1) * N // 2], w1_grouped[h][:])
+            return codes
 
         z_grouped = [
-            keep.tile([P, c1 - c0, PACK], BF16, name="z_grouped%d" % c, align_bytes=64)
-            for c, (c0, c1) in enumerate(CHUNKS)
+            keep.tile([P, c1 - c0, PACK], BF16, name="z_grouped%d" % k, align_bytes=64)
+            for k, (c0, c1) in enumerate(PARTS)
         ]
 
-        def write_pair(copy, t, c):
-            c0, c1 = CHUNKS[c]
-            copy(
-                out=z_grouped[c][:, :, t : t + 2],
-                in_=z[t][:].rearrange("p (r w) -> p w r", r=2)[:, c0:c1, :],
+        def write_pair(copy, t, k, c0, c1):
+            interleave(
+                copy,
+                z_grouped[k][:, c0 - PARTS[k][0] : c1 - PARTS[k][0], t : t + 2],
+                z[t][:].rearrange("p (r w) -> p r w", r=2)[:, :, c0:c1],
             )
 
-        for c in range(len(CHUNKS)):
-            write_pair(nc.scalar.copy, 0, c)
+        values = weigh(0, project(0, 0, H, 10240), 0, H)
+        round_w1(1)
+        stage(1)
+        scatter(0, 0, H, values)
+        active = project(2, 0, H, 12288)
+        values = weigh(2, active, 0, LAST_CUT)
+        stage(3)
+        scatter(2, 0, LAST_CUT, values)
+        round_w1(0)
+        w1_codes = [quantize_w1(0, "w1_codes0")]
+        for k in range(2):
+            write_pair(nc.scalar.copy, 0, k, *PARTS[k])
+        scatter(2, LAST_CUT, H, weigh(2, active, LAST_CUT, H))
+        for k in range(2, len(PARTS)):
+            write_pair(nc.scalar.copy, 0, k, *PARTS[k])
+        write_pair(nc.scalar.copy, 2, len(PARTS) - 1, *PARTS[-1])
 
         out_rows = out.rearrange("(mt p) w -> p mt w", p=P)
-        for first, last, tiles_a_store in STORES:
-            g0, g1 = CHUNKS[first][0], CHUNKS[last - 1][1]
-            result = keep.tile([P, N // P, g1 - g0], F32, name="result%d" % first, align_bytes=256)
-            for c in range(first, last):
-                c0, c1 = CHUNKS[c]
-                width = c1 - c0
-                z_codes = keep.tile([P, width], U32, name="z_codes%d" % c, align_bytes=64)
-                z_scales = keep.tile([P, width], U8, name="z_scales%d" % c, align_bytes=64)
-                write_pair(nc.vector.tensor_copy, 2, c)
-                quantize(z_codes[:], z_scales[:], z_grouped[c][:])
-                per_bank = 2 if c == 0 else BANK // width
-                for mt0 in range(0, N // P, per_bank):
-                    acc = psum.tile([P, BANK], F32, name="acc")
-                    for i in range(per_bank):
-                        mt = mt0 + i
-                        nc.tensor.matmul_mx(
-                            out=acc[:, i * width : (i + 1) * width],
-                            lhsT=w1_codes[:, mt * P : (mt + 1) * P].bitcast(FP8X4),
-                            lhsT_scale=w1_scales[:, mt * P : (mt + 1) * P],
-                            rhs=z_codes[:].bitcast(FP8X4),
-                            rhs_scale=z_scales[:],
-                            start=True,
-                            stop=True,
-                        )
-                    copy = nc.vector.tensor_copy if width == BANK and mt0 % 2 == 0 else nc.scalar.copy
-                    copy(
-                        out=result[:, mt0 : mt0 + per_bank, c0 - g0 : c1 - g0],
-                        in_=acc[:, 0 : per_bank * width].rearrange("p (a w) -> p a w", a=per_bank),
+
+        def empty(copy, acc, mt0, per_bank, c0, c1):
+            result = keep.tile([P, per_bank, c1 - c0], F32, name="result%d_%d" % (c0, mt0), align_bytes=256)
+            copy(out=result[:].rearrange("p a w -> p (a w)"), in_=acc[:, 0 : per_bank * (c1 - c0)])
+            nc.sync.dma_start(out_rows[:, mt0 : mt0 + per_bank, c0:c1], result[:])
+
+        late = []
+        for c, (k, c0, c1, per_bank) in enumerate(CHUNKS):
+            width = c1 - c0
+            z_codes = keep.tile([P, width], U32, name="z_codes%d" % c, align_bytes=64)
+            z_scales = keep.tile([P, width], U8, name="z_scales%d" % c, align_bytes=64)
+            if c < len(CHUNKS) - 1:
+                write_pair(nc.vector.tensor_copy, 2, k, c0, c1)
+            if c == 0:
+                w1_codes.append(quantize_w1(1, "values2_%d" % LAST_CUT))
+            quantize(z_codes[:], z_scales[:], z_grouped[k][:, c0 - PARTS[k][0] : c1 - PARTS[k][0], :])
+            for mt0 in range(0, N // P, per_bank):
+                acc = psum.tile([P, BANK], F32, name="acc")
+                for i in range(per_bank):
+                    mt = mt0 + i
+                    nc.tensor.matmul_mx(
+                        out=acc[:, i * width : (i + 1) * width],
+                        lhsT=w1_codes[mt // 2][:, mt % 2 * P : (mt % 2 + 1) * P].bitcast(FP8X4),
+                        lhsT_scale=w1_scales[:, mt * P : (mt + 1) * P],
+                        rhs=z_codes[:].bitcast(FP8X4),
+                        rhs_scale=z_scales[:],
+                        start=True,
+                        stop=True,
                     )
-                    if c == last - 1:
-                        for s0 in range(mt0, mt0 + per_bank, tiles_a_store):
-                            nc.sync.dma_start(
-                                out_rows[:, s0 : s0 + tiles_a_store, g0:g1], result[:, s0 : s0 + tiles_a_store, :]
-                            )
+                if (c, mt0) in ON_VECTOR:
+                    late.append((acc, mt0, per_bank, c0, c1))
+                else:
+                    empty(nc.scalar.copy, acc, mt0, per_bank, c0, c1)
+        for bank in late:
+            empty(nc.vector.tensor_copy, *bank)

@@ -23,9 +23,10 @@ BLOCKS = S // (PACK * RUN)
 LIST_ROWS = 16
 BANK = 512
 WA_PIECES = ((0, 128), (128, 256), (256, 512))
-PARTS = ((0, 256), (256, 512), (512, 768), (768, 1024))
-CHUNKS = ((0, 0, 128, 2), (0, 128, 256, 4), (1, 256, 512, 2), (2, 512, 768, 2), (3, 768, 1024, 2))
-ON_VECTOR = ((3, 0), (3, 2), (4, 2))
+PARTS = ((0, 384), (384, 512), (512, 768), (768, 1024))
+CHUNKS = ((0, 128, 2), (128, 384, 2), (384, 512, 4), (512, 1024, 1))
+STORES = ((0, 128), (128, 384), (384, 1024))
+ON_VECTOR = ((3, 0), (3, 2))
 LAST_CUT = 384
 
 
@@ -194,21 +195,36 @@ def tile_picked_blkmix_relu_p_kernel(
 
         out_rows = out.rearrange("(mt p) w -> p mt w", p=P)
 
+        results = [
+            keep.tile([P, N // P, g1 - g0], F32, name="result%d" % g0, align_bytes=256) for g0, g1 in STORES
+        ]
+
         def empty(copy, acc, mt0, per_bank, c0, c1):
-            result = keep.tile([P, per_bank, c1 - c0], F32, name="result%d_%d" % (c0, mt0), align_bytes=256)
-            copy(out=result[:].rearrange("p a w -> p (a w)"), in_=acc[:, 0 : per_bank * (c1 - c0)])
-            nc.sync.dma_start(out_rows[:, mt0 : mt0 + per_bank, c0:c1], result[:])
+            g = [c0 < g1 for g0, g1 in STORES].index(True)
+            g0, g1 = STORES[g]
+            tiles = slice(mt0, mt0 + per_bank)
+            copy(
+                out=results[g][:, tiles, c0 - g0 : c1 - g0],
+                in_=acc[:, 0 : per_bank * (c1 - c0)].rearrange("p (a w) -> p a w", a=per_bank),
+            )
+            if c1 == g1:
+                nc.sync.dma_start(out_rows[:, tiles, g0:g1], results[g][:, tiles, :])
 
         late = []
-        for c, (k, c0, c1, per_bank) in enumerate(CHUNKS):
+        for c, (c0, c1, per_bank) in enumerate(CHUNKS):
             width = c1 - c0
             z_codes = keep.tile([P, width], U32, name="z_codes%d" % c, align_bytes=64)
             z_scales = keep.tile([P, width], U8, name="z_scales%d" % c, align_bytes=64)
-            if c < len(CHUNKS) - 1:
-                write_pair(nc.vector.tensor_copy, 2, k, c0, c1)
-            if c == 0:
-                w1_codes.append(quantize_w1(1, "values2_%d" % LAST_CUT))
-            quantize(z_codes[:], z_scales[:], z_grouped[k][:, c0 - PARTS[k][0] : c1 - PARTS[k][0], :])
+            for k, (p0, p1) in enumerate(PARTS):
+                a0, a1 = max(c0, p0), min(c1, p1)
+                if a0 < a1:
+                    if k < len(PARTS) - 1:
+                        write_pair(nc.vector.tensor_copy, 2, k, a0, a1)
+                    if c == 0:
+                        w1_codes.append(quantize_w1(1, "values2_%d" % LAST_CUT))
+                    quantize(
+                        z_codes[:, a0 - c0 : a1 - c0], z_scales[:, a0 - c0 : a1 - c0], z_grouped[k][:, a0 - p0 : a1 - p0, :]
+                    )
             for mt0 in range(0, N // P, per_bank):
                 acc = psum.tile([P, BANK], F32, name="acc")
                 for i in range(per_bank):

@@ -15,6 +15,7 @@ FP8X4 = mybir.dt.float8_e4m3fn_x4
 RELU = mybir.ActivationFunctionType.Relu
 COPY = mybir.ActivationFunctionType.Copy
 MULT = mybir.AluOpType.mult
+ADD = mybir.AluOpType.add
 
 P = 128
 PACK = 4
@@ -157,7 +158,12 @@ def tile_picked_blkmix_relu_p_kernel(
         w1_scales = keep.tile([P, N], U8, name="w1_scales", align_bytes=64)
 
         def round_w1(h):
-            interleave(nc.scalar.copy, w1_grouped[h][:], w1_raw[:, :, h * N // 2 : (h + 1) * N // 2])
+            for m0 in range(0, N // 2, P):
+                interleave(
+                    lambda out, in_: nc.gpsimd.tensor_scalar(out, in_, 1.0, 0.0, MULT, ADD),
+                    w1_grouped[h][:, m0 : m0 + P, :],
+                    w1_raw[:, :, h * N // 2 + m0 : h * N // 2 + m0 + P],
+                )
 
         def quantize_w1(h, tag):
             codes = keep.tile([P, N // 2], U32, name="w1_codes%d" % h, tag=tag, align_bytes=256)
@@ -177,6 +183,7 @@ def tile_picked_blkmix_relu_p_kernel(
             )
 
         values = weigh(0, project(0, 0, H, 10240), 0, H)
+        round_w1(0)
         round_w1(1)
         stage(1)
         scatter(0, 0, H, values)
@@ -184,8 +191,7 @@ def tile_picked_blkmix_relu_p_kernel(
         values = weigh(2, active, 0, LAST_CUT)
         stage(3)
         scatter(2, 0, LAST_CUT, values)
-        round_w1(0)
-        w1_codes = [quantize_w1(0, "w1_codes0")]
+        w1_codes = [quantize_w1(0, "z3")]
         for k in range(2):
             write_pair(nc.scalar.copy, 0, k, *PARTS[k])
         scatter(2, LAST_CUT, H, weigh(2, active, LAST_CUT, H))

@@ -24,10 +24,21 @@ BLOCKS = S // (PACK * RUN)
 LIST_ROWS = 16
 BANK = 512
 WA_PIECES = ((0, 128), (128, 256), (256, 512))
-PARTS = ((0, 384), (384, 512), (512, 768), (768, 1024))
-CHUNKS = ((0, 128, 2), (128, 384, 2), (384, 512, 4), (512, 1024, 1))
-STORES = ((0, 128), (128, 384), (384, 1024))
-ON_VECTOR = ((3, 0), (3, 2))
+PARTS = ((0, 256), (256, 512), (512, 768), (768, 1024))
+HELPED = 1
+STEPS = ((0, 0, 128), (0, 128, 256), (1, 256, 512), (2, 512, 768), (3, 768, 1024))
+BANKS = (
+    (False, 0, 2, 0, 128),
+    (False, 2, 2, 0, 128),
+    (False, 0, 4, 128, 256),
+    (False, 0, 2, 256, 512),
+    (False, 2, 2, 256, 512),
+    (True, 0, 1, 512, 1024),
+    (False, 1, 1, 512, 1024),
+    (True, 2, 1, 512, 1024),
+    (True, 3, 1, 768, 1024),
+    (False, 3, 1, 512, 768),
+)
 LAST_CUT = 384
 
 
@@ -157,10 +168,13 @@ def tile_picked_blkmix_relu_p_kernel(
         w1_grouped = [keep.tile([P, N // 2, PACK], BF16, name="w1_grouped%d" % h, align_bytes=64) for h in range(2)]
         w1_scales = keep.tile([P, N], U8, name="w1_scales", align_bytes=64)
 
+        def gpsimd_copy(out, in_):
+            nc.gpsimd.tensor_scalar(out, in_, 1.0, 0.0, MULT, ADD)
+
         def round_w1(h):
             for m0 in range(0, N // 2, P):
                 interleave(
-                    lambda out, in_: nc.gpsimd.tensor_scalar(out, in_, 1.0, 0.0, MULT, ADD),
+                    gpsimd_copy,
                     w1_grouped[h][:, m0 : m0 + P, :],
                     w1_raw[:, :, h * N // 2 + m0 : h * N // 2 + m0 + P],
                 )
@@ -192,61 +206,62 @@ def tile_picked_blkmix_relu_p_kernel(
         stage(3)
         scatter(2, 0, LAST_CUT, values)
         w1_codes = [quantize_w1(0, "z3")]
-        for k in range(2):
+        for i in range(2):
+            unread = psum.tile([P, BANK], F32, name="acc")
+            nc.tensor.matmul_mx(
+                out=unread[:],
+                lhsT=w1_codes[0][:, i * P : (i + 1) * P].bitcast(FP8X4),
+                lhsT_scale=w1_scales[:, i * P : (i + 1) * P],
+                rhs=wa_codes[:].bitcast(FP8X4),
+                rhs_scale=wa_scales[:],
+                start=True,
+                stop=True,
+            )
+        write_pair(gpsimd_copy, 0, HELPED, *PARTS[HELPED])
+        for k in (0, 2):
             write_pair(nc.scalar.copy, 0, k, *PARTS[k])
         scatter(2, LAST_CUT, H, weigh(2, active, LAST_CUT, H))
-        for k in range(2, len(PARTS)):
-            write_pair(nc.scalar.copy, 0, k, *PARTS[k])
-        write_pair(nc.scalar.copy, 2, len(PARTS) - 1, *PARTS[-1])
+        write_pair(nc.scalar.copy, 0, 3, *PARTS[3])
+        write_pair(nc.scalar.copy, 2, HELPED, *PARTS[HELPED])
 
         out_rows = out.rearrange("(mt p) w -> p mt w", p=P)
 
-        results = [
-            keep.tile([P, N // P, g1 - g0], F32, name="result%d" % g0, align_bytes=256) for g0, g1 in STORES
-        ]
+        z_codes = keep.tile([P, U], U32, name="z_codes", align_bytes=64)
+        z_scales = keep.tile([P, U], U8, name="z_scales", align_bytes=64)
 
-        def empty(copy, acc, mt0, per_bank, c0, c1):
-            g = [c0 < g1 for g0, g1 in STORES].index(True)
-            g0, g1 = STORES[g]
-            tiles = slice(mt0, mt0 + per_bank)
-            copy(
-                out=results[g][:, tiles, c0 - g0 : c1 - g0],
-                in_=acc[:, 0 : per_bank * (c1 - c0)].rearrange("p (a w) -> p a w", a=per_bank),
-            )
-            if c1 == g1:
-                nc.sync.dma_start(out_rows[:, tiles, g0:g1], results[g][:, tiles, :])
+        def multiply(mt0, tiles, c0, c1):
+            acc = psum.tile([P, BANK], F32, name="acc")
+            for i in range(tiles):
+                mt = mt0 + i
+                nc.tensor.matmul_mx(
+                    out=acc[:, i * (c1 - c0) : (i + 1) * (c1 - c0)],
+                    lhsT=w1_codes[mt // 2][:, mt % 2 * P : (mt % 2 + 1) * P].bitcast(FP8X4),
+                    lhsT_scale=w1_scales[:, mt * P : (mt + 1) * P],
+                    rhs=z_codes[:, c0:c1].bitcast(FP8X4),
+                    rhs_scale=z_scales[:, c0:c1],
+                    start=True,
+                    stop=True,
+                )
+            return acc
+
+        def empty(copy, acc, mt0, tiles, c0, c1):
+            result = keep.tile([P, tiles, c1 - c0], F32, name="result%d_%d" % (c0, mt0), align_bytes=256)
+            copy(out=result[:].rearrange("p a w -> p (a w)"), in_=acc[:, 0 : tiles * (c1 - c0)])
+            nc.sync.dma_start(out_rows[:, mt0 : mt0 + tiles, c0:c1], result[:])
 
         late = []
-        for c, (c0, c1, per_bank) in enumerate(CHUNKS):
-            width = c1 - c0
-            z_codes = keep.tile([P, width], U32, name="z_codes%d" % c, align_bytes=64)
-            z_scales = keep.tile([P, width], U8, name="z_scales%d" % c, align_bytes=64)
-            for k, (p0, p1) in enumerate(PARTS):
-                a0, a1 = max(c0, p0), min(c1, p1)
-                if a0 < a1:
-                    if k < len(PARTS) - 1:
-                        write_pair(nc.vector.tensor_copy, 2, k, a0, a1)
-                    if c == 0:
-                        w1_codes.append(quantize_w1(1, "values2_%d" % LAST_CUT))
-                    quantize(
-                        z_codes[:, a0 - c0 : a1 - c0], z_scales[:, a0 - c0 : a1 - c0], z_grouped[k][:, a0 - p0 : a1 - p0, :]
-                    )
-            for mt0 in range(0, N // P, per_bank):
-                acc = psum.tile([P, BANK], F32, name="acc")
-                for i in range(per_bank):
-                    mt = mt0 + i
-                    nc.tensor.matmul_mx(
-                        out=acc[:, i * width : (i + 1) * width],
-                        lhsT=w1_codes[mt // 2][:, mt % 2 * P : (mt % 2 + 1) * P].bitcast(FP8X4),
-                        lhsT_scale=w1_scales[:, mt * P : (mt + 1) * P],
-                        rhs=z_codes[:].bitcast(FP8X4),
-                        rhs_scale=z_scales[:],
-                        start=True,
-                        stop=True,
-                    )
-                if (c, mt0) in ON_VECTOR:
-                    late.append((acc, mt0, per_bank, c0, c1))
-                else:
-                    empty(nc.scalar.copy, acc, mt0, per_bank, c0, c1)
+        for k, q0, q1 in STEPS:
+            if k != HELPED:
+                write_pair(nc.vector.tensor_copy, 2, k, q0, q1)
+            if q0 == 0:
+                w1_codes.append(quantize_w1(1, "values2_%d" % LAST_CUT))
+            quantize(z_codes[:, q0:q1], z_scales[:, q0:q1], z_grouped[k][:, q0 - PARTS[k][0] : q1 - PARTS[k][0], :])
+            for on_vector, mt0, tiles, c0, c1 in BANKS:
+                if q0 < c1 <= q1:
+                    acc = multiply(mt0, tiles, c0, c1)
+                    if on_vector:
+                        late.append((acc, mt0, tiles, c0, c1))
+                    else:
+                        empty(nc.scalar.copy, acc, mt0, tiles, c0, c1)
         for bank in late:
             empty(nc.vector.tensor_copy, *bank)

@@ -78,10 +78,10 @@ def tile_picked_blkmix_relu_p_kernel(
 
         load_wa(0)
         nc.sync.dma_start(picks[:], offs)
-        for q in range(4):
+        for r in range(4):
             nc.sync.dma_start(
-                table_scales[32 * q : 32 * q + 4, :].bitcast(I32),
-                x_scales[0, 4 * q : 4 * q + 4, :].bitcast(I32),
+                table_scales[r:P:32, :].bitcast(I32),
+                x_scales[0, r:16:4, :].bitcast(I32),
             )
         nc.sync.dma_start(table_words[:], x_words[0].rearrange("p n t -> p (n t)").bitcast(I32))
         load_wa(1)

@@ -28,16 +28,17 @@ PARTS = ((0, 256), (256, 512), (512, 768), (768, 1024))
 HELPED = 1
 STEPS = ((0, 0, 128), (0, 128, 256), (1, 256, 512), (2, 512, 768), (3, 768, 1024))
 BANKS = (
-    (False, 0, 2, 0, 128),
-    (False, 2, 2, 0, 128),
-    (False, 0, 4, 128, 256),
+    (False, 0, 1, 0, 128),
+    (False, 1, 1, 0, 128),
+    (False, 2, 1, 0, 256),
+    (False, 0, 2, 128, 256),
+    (False, 3, 1, 0, 512),
     (False, 0, 2, 256, 512),
-    (False, 2, 2, 256, 512),
+    (False, 2, 1, 256, 512),
     (True, 0, 1, 512, 1024),
     (False, 1, 1, 512, 1024),
     (True, 2, 1, 512, 1024),
-    (True, 3, 1, 768, 1024),
-    (False, 3, 1, 512, 768),
+    (False, 3, 1, 512, 1024),
 )
 LAST_CUT = 384
 

@@ -30,11 +30,14 @@ STEPS = ((0, 0, 128), (0, 128, 256), (1, 256, 512), (2, 512, 768), (3, 768, 1024
 BANKS = (
     (False, 0, 1, 0, 128),
     (False, 1, 1, 0, 128),
-    (False, 2, 1, 0, 256),
+    (False, 2, 1, 0, 128),
+    (False, 3, 1, 0, 128),
     (False, 0, 2, 128, 256),
-    (False, 3, 1, 0, 512),
-    (False, 0, 2, 256, 512),
+    (False, 2, 2, 128, 256),
+    (False, 0, 1, 256, 512),
+    (False, 1, 1, 256, 512),
     (False, 2, 1, 256, 512),
+    (False, 3, 1, 256, 512),
     (True, 0, 1, 512, 1024),
     (False, 1, 1, 512, 1024),
     (True, 2, 1, 512, 1024),

@@ -43,7 +43,7 @@ BANKS = (
     (True, 2, 1, 512, 1024),
     (False, 3, 1, 512, 1024),
 )
-LAST_CUT = 384
+LAST_CUT = 320
 
 
 def interleave(copy, grouped, raw):
@@ -169,24 +169,15 @@ def tile_picked_blkmix_relu_p_kernel(
         def stage(t):
             nc.scalar.activation(out=z[t - 1][:, U : 2 * U], in_=z[t][:], func=COPY, scale=gate[t][:])
 
-        w1_grouped = [keep.tile([P, N // 2, PACK], BF16, name="w1_grouped%d" % h, align_bytes=64) for h in range(2)]
+        w1_grouped = keep.tile([P, N, PACK], BF16, name="w1_grouped", align_bytes=64)
         w1_scales = keep.tile([P, N], U8, name="w1_scales", align_bytes=64)
 
         def gpsimd_copy(out, in_):
             nc.gpsimd.tensor_scalar(out, in_, 1.0, 0.0, MULT, ADD)
 
-        def round_w1(h):
-            for m0 in range(0, N // 2, P):
-                interleave(
-                    gpsimd_copy,
-                    w1_grouped[h][:, m0 : m0 + P, :],
-                    w1_raw[:, :, h * N // 2 + m0 : h * N // 2 + m0 + P],
-                )
-
-        def quantize_w1(h, tag):
-            codes = keep.tile([P, N // 2], U32, name="w1_codes%d" % h, tag=tag, align_bytes=256)
-            quantize(codes[:], w1_scales[:, h * N // 2 : (h + 1) * N // 2], w1_grouped[h][:])
-            return codes
+        def quantize_w1(m0, m1, codes):
+            quantize(codes[:], w1_scales[:, m0:m1], w1_grouped[:, m0:m1, :])
+            return [codes[:, m : m + P] for m in range(0, m1 - m0, P)]
 
         z_grouped = [
             keep.tile([P, c1 - c0, PACK], BF16, name="z_grouped%d" % k, align_bytes=64)
@@ -201,31 +192,32 @@ def tile_picked_blkmix_relu_p_kernel(
             )
 
         values = weigh(0, project(0, 0, H, 10240), 0, H)
-        round_w1(0)
-        round_w1(1)
+        for m0 in range(0, N, P):
+            interleave(gpsimd_copy, w1_grouped[:, m0 : m0 + P, :], w1_raw[:, :, m0 : m0 + P])
         stage(1)
         scatter(0, 0, H, values)
         active = project(2, 0, H, 12288)
         values = weigh(2, active, 0, LAST_CUT)
         stage(3)
         scatter(2, 0, LAST_CUT, values)
-        w1_codes = [quantize_w1(0, "z3")]
-        for i in range(2):
+        w1_codes = quantize_w1(0, P, keep.tile([P, P], U32, name="w1_codes0", tag="z3", align_bytes=256))
+        for i in range(3):
             unread = psum.tile([P, BANK], F32, name="acc")
             nc.tensor.matmul_mx(
                 out=unread[:],
-                lhsT=w1_codes[0][:, i * P : (i + 1) * P].bitcast(FP8X4),
-                lhsT_scale=w1_scales[:, i * P : (i + 1) * P],
+                lhsT=w1_codes[0].bitcast(FP8X4),
+                lhsT_scale=w1_scales[:, 0:P],
                 rhs=wa_codes[:].bitcast(FP8X4),
                 rhs_scale=wa_scales[:],
                 start=True,
                 stop=True,
             )
         write_pair(gpsimd_copy, 0, HELPED, *PARTS[HELPED])
-        for k in (0, 2):
-            write_pair(nc.scalar.copy, 0, k, *PARTS[k])
+        write_pair(nc.scalar.copy, 0, 0, *PARTS[0])
         scatter(2, LAST_CUT, H, weigh(2, active, LAST_CUT, H))
-        write_pair(nc.scalar.copy, 0, 3, *PARTS[3])
+        w1_codes += quantize_w1(P, 2 * P, shared.tile([P, P], U32, name="w1_codes1", align_bytes=256, offset=12288))
+        for k in (2, 3):
+            write_pair(nc.scalar.copy, 0, k, *PARTS[k])
         write_pair(nc.scalar.copy, 2, HELPED, *PARTS[HELPED])
 
         out_rows = out.rearrange("(mt p) w -> p mt w", p=P)
@@ -239,7 +231,7 @@ def tile_picked_blkmix_relu_p_kernel(
                 mt = mt0 + i
                 nc.tensor.matmul_mx(
                     out=acc[:, i * (c1 - c0) : (i + 1) * (c1 - c0)],
-                    lhsT=w1_codes[mt // 2][:, mt % 2 * P : (mt % 2 + 1) * P].bitcast(FP8X4),
+                    lhsT=w1_codes[mt].bitcast(FP8X4),
                     lhsT_scale=w1_scales[:, mt * P : (mt + 1) * P],
                     rhs=z_codes[:, c0:c1].bitcast(FP8X4),
                     rhs_scale=z_scales[:, c0:c1],
@@ -258,7 +250,8 @@ def tile_picked_blkmix_relu_p_kernel(
             if k != HELPED:
                 write_pair(nc.vector.tensor_copy, 2, k, q0, q1)
             if q0 == 0:
-                w1_codes.append(quantize_w1(1, "values2_%d" % LAST_CUT))
+                codes = keep.tile([P, 2 * P], U32, name="w1_codes2", tag="values2_%d" % LAST_CUT, align_bytes=256)
+                w1_codes += quantize_w1(2 * P, N, codes)
             quantize(z_codes[:, q0:q1], z_scales[:, q0:q1], z_grouped[k][:, q0 - PARTS[k][0] : q1 - PARTS[k][0], :])
             for on_vector, mt0, tiles, c0, c1 in BANKS:
                 if q0 < c1 <= q1:

@@ -23,27 +23,14 @@ RUN = 8
 BLOCKS = S // (PACK * RUN)
 LIST_ROWS = 16
 BANK = 512
-WA_PIECES = ((0, 128), (128, 256), (256, 512))
+TABLE_FIRST = 512
+PIECES = ((0, 128), (128, 256), (256, 512))
+LAST_CUT = 384
+WARM_UPS = 2
 PARTS = ((0, 256), (256, 512), (512, 768), (768, 1024))
 HELPED = 1
 STEPS = ((0, 0, 128), (0, 128, 256), (1, 256, 512), (2, 512, 768), (3, 768, 1024))
-BANKS = (
-    (False, 0, 1, 0, 128),
-    (False, 1, 1, 0, 128),
-    (False, 2, 1, 0, 128),
-    (False, 3, 1, 0, 128),
-    (False, 0, 2, 128, 256),
-    (False, 2, 2, 128, 256),
-    (False, 0, 1, 256, 512),
-    (False, 1, 1, 256, 512),
-    (False, 2, 1, 256, 512),
-    (False, 3, 1, 256, 512),
-    (True, 0, 1, 512, 1024),
-    (False, 1, 1, 512, 1024),
-    (True, 2, 1, 512, 1024),
-    (False, 3, 1, 512, 1024),
-)
-LAST_CUT = 320
+STORES = ((0, 128, 1), (128, 256, 2), (256, 512, 1), (512, 1024, 1))
 
 
 def interleave(copy, grouped, raw):
@@ -62,70 +49,68 @@ def tile_picked_blkmix_relu_p_kernel(
         shared = ctx.enter_context(tc.tile_pool(name="shared", bufs=1))
         psum = ctx.enter_context(tc.psum_pool(name="psum", bufs=8))
 
-        picks = keep.tile([P, S // LIST_ROWS], U16, name="picks")
-        places = keep.tile([P, H // LIST_ROWS], U16, name="places")
-        table_words = keep.tile([P, T], I32, name="table_words", align_bytes=256)
-        table_scales = keep.tile([P, T], U8, name="table_scales", align_bytes=64)
-        gate = [keep.tile([P, 1], F32, name="gate%d" % t) for t in range(PACK)]
-        wa_rows = wa.rearrange("(p j) h -> p j h", j=PACK)
-        wa_raw = [
-            shared.tile([P, PACK, h1 - h0], F32, name="wa_raw%d" % i, align_bytes=256, offset=16 * h0)
-            for i, (h0, h1) in enumerate(WA_PIECES)
-        ]
-        w1_raw = keep.tile([P, PACK, N], F32, name="w1_raw", align_bytes=256)
-
-        nc.vector.memset(table_scales[:].bitcast(I32), 0)
-
-        def load_wa(i):
-            h0, h1 = WA_PIECES[i]
-            nc.sync.dma_start(wa_raw[i][:], wa_rows[:, :, h0:h1])
-
-        load_wa(0)
-        nc.sync.dma_start(picks[:], offs)
-        for r in range(4):
-            nc.sync.dma_start(
-                table_scales[r:P:32, :].bitcast(I32),
-                x_scales[0, r:16:4, :].bitcast(I32),
-            )
-        nc.sync.dma_start(table_words[:], x_words[0].rearrange("p n t -> p (n t)").bitcast(I32))
-        load_wa(1)
-        nc.sync.dma_start(places[:], fl)
-        load_wa(2)
-        gt_rows = gt.rearrange("(b t q) o -> t b q o", t=PACK, q=RUN)
-        w1_rows = w1.rearrange("(b t q) m -> t b q m", t=PACK, q=RUN)
-        for t in range(PACK):
-            nc.sync.dma_start(w1_raw[:, t, :], w1_rows[t])
-        for t in range(PACK):
-            nc.sync.dma_start(gate[t][:], gt_rows[t])
-
-        z = [keep.tile([P, U if t % 2 else 2 * U], F32, name="z%d" % t, align_bytes=256) for t in range(PACK)]
-        for t in (1, 3):
-            nc.vector.memset(z[t][:], 0.0)
-        for t in (0, 2):
-            nc.scalar.activation(out=z[t][:, 0:U], in_=z[t + 1][:], func=COPY)
-
-        wa_grouped = [
-            keep.tile([P, h1 - h0, PACK], BF16, name="wa_grouped%d" % i, tag="wa_grouped%d" % min(i, 1), align_bytes=64)
-            for i, (h0, h1) in enumerate(WA_PIECES)
-        ]
-        wa_codes = keep.tile([P, H], U32, name="wa_codes", align_bytes=64)
-        wa_scales = keep.tile([P, H], U8, name="wa_scales", align_bytes=64)
+        def held(shape, dtype, name, tag=None):
+            return keep.tile(shape, dtype, name=name, tag=tag or name, align_bytes=256)
 
         def quantize(codes, scales, grouped):
             nc.vector.quantize_mx(
                 out=codes.bitcast(FP8X4), scales=scales, in_=grouped.rearrange("p w j -> p (w j)")
             )
 
-        def prepare_wa(i):
-            h0, h1 = WA_PIECES[i]
-            interleave(nc.scalar.copy, wa_grouped[i][:], wa_raw[i][:])
-            quantize(wa_codes[:, h0:h1], wa_scales[:, h0:h1], wa_grouped[i][:])
+        def product(acc, lhs, lhs_scale, rhs, rhs_scale):
+            nc.tensor.matmul_mx(
+                out=acc,
+                lhsT=lhs.bitcast(FP8X4),
+                lhsT_scale=lhs_scale,
+                rhs=rhs.bitcast(FP8X4),
+                rhs_scale=rhs_scale,
+                start=True,
+                stop=True,
+            )
 
-        picked_scales = keep.tile([P, S], U8, name="picked_scales", align_bytes=64)
-        x_scale_plane = keep.tile([P, S], U8, name="x_scale_plane", align_bytes=64)
-        x_codes = keep.tile([P, S], U32, name="x_codes", align_bytes=64)
+        def gpsimd_copy(out, in_):
+            nc.gpsimd.tensor_scalar(out, in_, 1.0, 0.0, MULT, ADD)
+
+        picks = keep.tile([P, S // LIST_ROWS], U16, name="picks")
+        places = keep.tile([P, H // LIST_ROWS], U16, name="places")
+        table_words = held([P, T], I32, "table_words")
+        table_scales = held([P, T], U8, "table_scales")
+        gate = [keep.tile([P, 1], F32, name="gate%d" % t) for t in range(PACK)]
+        wa_raw = [
+            shared.tile([P, PACK, h1 - h0], F32, name="wa_raw%d" % i, align_bytes=256, offset=16 * h0)
+            for i, (h0, h1) in enumerate(PIECES)
+        ]
+        w1_raw = held([P, PACK, N], F32, "w1_raw")
+
+        nc.vector.memset(table_scales[:].bitcast(I32), 0)
+        words = x_words[0].rearrange("p n t -> p (n t)").bitcast(I32)
+        wa_rows = wa.rearrange("(p j) h -> p j h", j=PACK)
+        gt_rows = gt.rearrange("(b t q) o -> t b q o", t=PACK, q=RUN)
+        w1_rows = w1.rearrange("(b t q) m -> t b q m", t=PACK, q=RUN)
+        nc.sync.dma_start(table_words[:, 0:TABLE_FIRST], words[:, 0:TABLE_FIRST])
+        nc.sync.dma_start(picks[:], offs)
+        for r in range(4):
+            nc.sync.dma_start(table_scales[r:P:32, :].bitcast(I32), x_scales[0, r:16:4, :].bitcast(I32))
+        nc.sync.dma_start(table_words[:, TABLE_FIRST:T], words[:, TABLE_FIRST:T])
+        for i, (h0, h1) in enumerate(PIECES):
+            nc.sync.dma_start(wa_raw[i][:], wa_rows[:, :, h0:h1])
+            if i == 1:
+                nc.sync.dma_start(places[:], fl)
+        for t in range(PACK):
+            nc.sync.dma_start(w1_raw[:, t, :], w1_rows[t])
+        for t in range(PACK):
+            nc.sync.dma_start(gate[t][:], gt_rows[t])
+
+        z = [held([P, U if t % 2 else 2 * U], F32, "z%d" % t) for t in range(PACK)]
+        for t in (1, 3):
+            nc.vector.memset(z[t][:], 0.0)
+        for t in (0, 2):
+            nc.scalar.activation(out=z[t][:, 0:U], in_=z[t + 1][:], func=COPY)
+
+        picked_scales = held([P, S], U8, "picked_scales")
+        x_scale_plane = held([P, S], U8, "x_scale_plane")
+        x_codes = held([P, S], U32, "x_codes")
         nc.vector.tensor_copy(picked_scales[:], table_scales[:].indirect(picks[:]))
-        prepare_wa(0)
         nc.vector.tensor_copy(
             x_scale_plane[:].bitcast(I32).rearrange("p (t b w) -> p t b w", t=PACK, b=BLOCKS),
             picked_scales[:].bitcast(I32).rearrange("p (b t w) -> p t b w", t=PACK, b=BLOCKS),
@@ -135,54 +120,56 @@ def tile_picked_blkmix_relu_p_kernel(
             table_words[:].bitcast(U32).indirect(picks[:]),
         )
 
-        def project(t, h0, h1, place):
+        wa_codes = held([P, H], U32, "wa_codes")
+        wa_scales = held([P, H], U8, "wa_scales")
+
+        def prepare_wa(i):
+            h0, h1 = PIECES[i]
+            grouped = held([P, h1 - h0, PACK], BF16, "wa_grouped%d" % i, "wa_grouped%d" % min(i, 1))
+            interleave(nc.scalar.copy, grouped[:], wa_raw[i][:])
+            quantize(wa_codes[:, h0:h1], wa_scales[:, h0:h1], grouped[:])
+
+        def project(t, h0, h1, offset):
             acc = psum.tile([P, BANK], F32, name="acc")
-            nc.tensor.matmul_mx(
-                out=acc[:, 0 : h1 - h0],
-                lhsT=x_codes[:, t * P : (t + 1) * P].bitcast(FP8X4),
-                lhsT_scale=x_scale_plane[:, t * P : (t + 1) * P],
-                rhs=wa_codes[:, h0:h1].bitcast(FP8X4),
-                rhs_scale=wa_scales[:, h0:h1],
-                start=True,
-                stop=True,
-            )
-            active = shared.tile([P, h1 - h0], F32, name="active%d_%d" % (t, h0), align_bytes=256, offset=place)
+            cols = slice(t * P, (t + 1) * P)
+            product(acc[:, 0 : h1 - h0], x_codes[:, cols], x_scale_plane[:, cols], wa_codes[:, h0:h1], wa_scales[:, h0:h1])
+            active = shared.tile([P, h1 - h0], F32, name="active%d_%d" % (t, h0), align_bytes=256, offset=offset)
             nc.scalar.activation(out=active[:], in_=acc[:, 0 : h1 - h0], func=RELU)
             return active
+
+        def weigh(t, active, name):
+            values = held(list(active.shape), F32, name)
+            nc.scalar.activation(out=values[:], in_=active, func=COPY, scale=gate[t][:])
+            return values
 
         def scatter(t, h0, h1, values):
             nc.vector.tensor_copy(z[t][:].indirect(places[:, h0 // LIST_ROWS : h1 // LIST_ROWS]), values[:])
 
-        prepare_wa(1)
-        places_of = {(1, 0): 2048, (3, 0): 2560, (1, 1): 4096, (3, 1): 4608, (1, 2): 8192, (3, 2): 9216}
-        for i, (h0, h1) in enumerate(WA_PIECES):
-            for t in (1, 3):
-                if (t, i) == (1, 1):
-                    prepare_wa(2)
-                scatter(t, h0, h1, project(t, h0, h1, places_of[(t, i)]))
-
-        def weigh(t, active, h0, h1):
-            values = keep.tile([P, h1 - h0], F32, name="values%d_%d" % (t, h0), align_bytes=256)
-            nc.scalar.activation(out=values[:], in_=active[:, h0:h1], func=COPY, scale=gate[t][:])
-            return values
-
         def stage(t):
             nc.scalar.activation(out=z[t - 1][:, U : 2 * U], in_=z[t][:], func=COPY, scale=gate[t][:])
 
-        w1_grouped = keep.tile([P, N, PACK], BF16, name="w1_grouped", align_bytes=64)
-        w1_scales = keep.tile([P, N], U8, name="w1_scales", align_bytes=64)
+        prepare_wa(0)
+        prepare_wa(1)
+        for i, (h0, h1) in enumerate(PIECES):
+            if i == 1:
+                prepare_wa(2)
+            for n, t in enumerate((1, 3)):
+                scatter(t, h0, h1, project(t, h0, h1, 16 * h1 + 4 * n * (h1 - h0)))
+        values = weigh(0, project(0, 0, H, 20 * H)[:], "values0")
+        stage(1)
+        scatter(0, 0, H, values)
 
-        def gpsimd_copy(out, in_):
-            nc.gpsimd.tensor_scalar(out, in_, 1.0, 0.0, MULT, ADD)
+        w1_grouped = held([P, N, PACK], BF16, "w1_grouped")
+        w1_scales = held([P, N], U8, "w1_scales")
+        for m0 in range(0, N, P):
+            interleave(gpsimd_copy, w1_grouped[:, m0 : m0 + P, :], w1_raw[:, :, m0 : m0 + P])
 
-        def quantize_w1(m0, m1, codes):
+        def quantize_w1(m0, m1, tag):
+            codes = held([P, m1 - m0], U32, "w1_codes%d" % m0, tag)
             quantize(codes[:], w1_scales[:, m0:m1], w1_grouped[:, m0:m1, :])
             return [codes[:, m : m + P] for m in range(0, m1 - m0, P)]
 
-        z_grouped = [
-            keep.tile([P, c1 - c0, PACK], BF16, name="z_grouped%d" % k, align_bytes=64)
-            for k, (c0, c1) in enumerate(PARTS)
-        ]
+        z_grouped = [held([P, c1 - c0, PACK], BF16, "z_grouped%d" % k) for k, (c0, c1) in enumerate(PARTS)]
 
         def write_pair(copy, t, k, c0, c1):
             interleave(
@@ -191,74 +178,46 @@ def tile_picked_blkmix_relu_p_kernel(
                 z[t][:].rearrange("p (r w) -> p r w", r=2)[:, :, c0:c1],
             )
 
-        values = weigh(0, project(0, 0, H, 10240), 0, H)
-        for m0 in range(0, N, P):
-            interleave(gpsimd_copy, w1_grouped[:, m0 : m0 + P, :], w1_raw[:, :, m0 : m0 + P])
-        stage(1)
-        scatter(0, 0, H, values)
-        active = project(2, 0, H, 12288)
-        values = weigh(2, active, 0, LAST_CUT)
+        active = project(2, 0, H, 24 * H)
+        values = weigh(2, active[:, 0:LAST_CUT], "values2_first")
         stage(3)
         scatter(2, 0, LAST_CUT, values)
-        w1_codes = quantize_w1(0, P, keep.tile([P, P], U32, name="w1_codes0", tag="z3", align_bytes=256))
-        for i in range(3):
+        w1_codes = quantize_w1(0, 2 * P, "z3")
+        for i in range(WARM_UPS):
             unread = psum.tile([P, BANK], F32, name="acc")
-            nc.tensor.matmul_mx(
-                out=unread[:],
-                lhsT=w1_codes[0].bitcast(FP8X4),
-                lhsT_scale=w1_scales[:, 0:P],
-                rhs=wa_codes[:].bitcast(FP8X4),
-                rhs_scale=wa_scales[:],
-                start=True,
-                stop=True,
-            )
+            product(unread[:], w1_codes[i], w1_scales[:, i * P : (i + 1) * P], wa_codes[:], wa_scales[:])
         write_pair(gpsimd_copy, 0, HELPED, *PARTS[HELPED])
-        write_pair(nc.scalar.copy, 0, 0, *PARTS[0])
-        scatter(2, LAST_CUT, H, weigh(2, active, LAST_CUT, H))
-        w1_codes += quantize_w1(P, 2 * P, shared.tile([P, P], U32, name="w1_codes1", align_bytes=256, offset=12288))
-        for k in (2, 3):
+        for k in (0, 2):
             write_pair(nc.scalar.copy, 0, k, *PARTS[k])
+        scatter(2, LAST_CUT, H, weigh(2, active[:, LAST_CUT:H], "values2_last"))
+        write_pair(nc.scalar.copy, 0, 3, *PARTS[3])
         write_pair(nc.scalar.copy, 2, HELPED, *PARTS[HELPED])
 
         out_rows = out.rearrange("(mt p) w -> p mt w", p=P)
-
-        z_codes = keep.tile([P, U], U32, name="z_codes", align_bytes=64)
-        z_scales = keep.tile([P, U], U8, name="z_scales", align_bytes=64)
-
-        def multiply(mt0, tiles, c0, c1):
-            acc = psum.tile([P, BANK], F32, name="acc")
-            for i in range(tiles):
-                mt = mt0 + i
-                nc.tensor.matmul_mx(
-                    out=acc[:, i * (c1 - c0) : (i + 1) * (c1 - c0)],
-                    lhsT=w1_codes[mt].bitcast(FP8X4),
-                    lhsT_scale=w1_scales[:, mt * P : (mt + 1) * P],
-                    rhs=z_codes[:, c0:c1].bitcast(FP8X4),
-                    rhs_scale=z_scales[:, c0:c1],
-                    start=True,
-                    stop=True,
-                )
-            return acc
-
-        def empty(copy, acc, mt0, tiles, c0, c1):
-            result = keep.tile([P, tiles, c1 - c0], F32, name="result%d_%d" % (c0, mt0), align_bytes=256)
-            copy(out=result[:].rearrange("p a w -> p (a w)"), in_=acc[:, 0 : tiles * (c1 - c0)])
-            nc.sync.dma_start(out_rows[:, mt0 : mt0 + tiles, c0:c1], result[:])
-
-        late = []
+        z_codes = held([P, U], U32, "z_codes")
+        z_scales = held([P, U], U8, "z_scales")
         for k, q0, q1 in STEPS:
             if k != HELPED:
                 write_pair(nc.vector.tensor_copy, 2, k, q0, q1)
             if q0 == 0:
-                codes = keep.tile([P, 2 * P], U32, name="w1_codes2", tag="values2_%d" % LAST_CUT, align_bytes=256)
-                w1_codes += quantize_w1(2 * P, N, codes)
+                w1_codes += quantize_w1(2 * P, N, "values2_last")
             quantize(z_codes[:, q0:q1], z_scales[:, q0:q1], z_grouped[k][:, q0 - PARTS[k][0] : q1 - PARTS[k][0], :])
-            for on_vector, mt0, tiles, c0, c1 in BANKS:
-                if q0 < c1 <= q1:
-                    acc = multiply(mt0, tiles, c0, c1)
-                    if on_vector:
-                        late.append((acc, mt0, tiles, c0, c1))
-                    else:
-                        empty(nc.scalar.copy, acc, mt0, tiles, c0, c1)
-        for bank in late:
-            empty(nc.vector.tensor_copy, *bank)
+            for c0, c1, tiles in STORES:
+                if c1 != q1:
+                    continue
+                width = c1 - c0
+                for mt0 in range(0, N // P, tiles):
+                    acc = psum.tile([P, BANK], F32, name="acc")
+                    for i in range(tiles):
+                        rows = slice((mt0 + i) * P, (mt0 + i + 1) * P)
+                        product(
+                            acc[:, i * width : (i + 1) * width],
+                            w1_codes[mt0 + i],
+                            w1_scales[:, rows],
+                            z_codes[:, c0:c1],
+                            z_scales[:, c0:c1],
+                        )
+                    result = held([P, tiles, width], F32, "result%d_%d" % (c0, mt0))
+                    copy = nc.vector.tensor_copy if c1 == U and mt0 % 2 == 0 else nc.scalar.copy
+                    copy(out=result[:].rearrange("p a w -> p (a w)"), in_=acc[:, 0 : tiles * width])
+                    nc.sync.dma_start(out_rows[:, mt0 : mt0 + tiles, c0:c1], result[:])

@@ -23,14 +23,13 @@ RUN = 8
 BLOCKS = S // (PACK * RUN)
 LIST_ROWS = 16
 BANK = 512
-TABLE_FIRST = 512
 PIECES = ((0, 128), (128, 256), (256, 512))
 LAST_CUT = 384
 WARM_UPS = 2
 PARTS = ((0, 256), (256, 512), (512, 768), (768, 1024))
 HELPED = 1
 STEPS = ((0, 0, 128), (0, 128, 256), (1, 256, 512), (2, 512, 768), (3, 768, 1024))
-STORES = ((0, 128, 1), (128, 256, 2), (256, 512, 1), (512, 1024, 1))
+STORES = ((0, 128, 1), (128, 256, 2), (256, 512, 1), (512, 768, 2), (768, 1024, 2))
 
 
 def interleave(copy, grouped, raw):
@@ -87,12 +86,12 @@ def tile_picked_blkmix_relu_p_kernel(
         wa_rows = wa.rearrange("(p j) h -> p j h", j=PACK)
         gt_rows = gt.rearrange("(b t q) o -> t b q o", t=PACK, q=RUN)
         w1_rows = w1.rearrange("(b t q) m -> t b q m", t=PACK, q=RUN)
-        nc.sync.dma_start(table_words[:, 0:TABLE_FIRST], words[:, 0:TABLE_FIRST])
+        nc.sync.dma_start(wa_raw[0][:], wa_rows[:, :, 0 : PIECES[0][1]])
         nc.sync.dma_start(picks[:], offs)
         for r in range(4):
             nc.sync.dma_start(table_scales[r:P:32, :].bitcast(I32), x_scales[0, r:16:4, :].bitcast(I32))
-        nc.sync.dma_start(table_words[:, TABLE_FIRST:T], words[:, TABLE_FIRST:T])
-        for i, (h0, h1) in enumerate(PIECES):
+        nc.sync.dma_start(table_words[:], words)
+        for i, (h0, h1) in list(enumerate(PIECES))[1:]:
             nc.sync.dma_start(wa_raw[i][:], wa_rows[:, :, h0:h1])
             if i == 1:
                 nc.sync.dma_start(places[:], fl)
@@ -107,19 +106,6 @@ def tile_picked_blkmix_relu_p_kernel(
         for t in (0, 2):
             nc.scalar.activation(out=z[t][:, 0:U], in_=z[t + 1][:], func=COPY)
 
-        picked_scales = held([P, S], U8, "picked_scales")
-        x_scale_plane = held([P, S], U8, "x_scale_plane")
-        x_codes = held([P, S], U32, "x_codes")
-        nc.vector.tensor_copy(picked_scales[:], table_scales[:].indirect(picks[:]))
-        nc.vector.tensor_copy(
-            x_scale_plane[:].bitcast(I32).rearrange("p (t b w) -> p t b w", t=PACK, b=BLOCKS),
-            picked_scales[:].bitcast(I32).rearrange("p (b t w) -> p t b w", t=PACK, b=BLOCKS),
-        )
-        nc.vector.tensor_copy(
-            x_codes[:].rearrange("p (t b q) -> p b t q", t=PACK, q=RUN),
-            table_words[:].bitcast(U32).indirect(picks[:]),
-        )
-
         wa_codes = held([P, H], U32, "wa_codes")
         wa_scales = held([P, H], U8, "wa_scales")
 
@@ -128,6 +114,20 @@ def tile_picked_blkmix_relu_p_kernel(
             grouped = held([P, h1 - h0, PACK], BF16, "wa_grouped%d" % i, "wa_grouped%d" % min(i, 1))
             interleave(nc.scalar.copy, grouped[:], wa_raw[i][:])
             quantize(wa_codes[:, h0:h1], wa_scales[:, h0:h1], grouped[:])
+
+        picked_scales = held([P, S], U8, "picked_scales")
+        x_scale_plane = held([P, S], U8, "x_scale_plane")
+        x_codes = held([P, S], U32, "x_codes")
+        nc.vector.tensor_copy(picked_scales[:], table_scales[:].indirect(picks[:]))
+        prepare_wa(0)
+        nc.vector.tensor_copy(
+            x_scale_plane[:].bitcast(I32).rearrange("p (t b w) -> p t b w", t=PACK, b=BLOCKS),
+            picked_scales[:].bitcast(I32).rearrange("p (b t w) -> p t b w", t=PACK, b=BLOCKS),
+        )
+        nc.vector.tensor_copy(
+            x_codes[:].rearrange("p (t b q) -> p b t q", t=PACK, q=RUN),
+            table_words[:].bitcast(U32).indirect(picks[:]),
+        )
 
         def project(t, h0, h1, offset):
             acc = psum.tile([P, BANK], F32, name="acc")
@@ -148,7 +148,6 @@ def tile_picked_blkmix_relu_p_kernel(
         def stage(t):
             nc.scalar.activation(out=z[t - 1][:, U : 2 * U], in_=z[t][:], func=COPY, scale=gate[t][:])
 
-        prepare_wa(0)
         prepare_wa(1)
         for i, (h0, h1) in enumerate(PIECES):
             if i == 1:
@@ -218,6 +217,6 @@ def tile_picked_blkmix_relu_p_kernel(
                             z_scales[:, c0:c1],
                         )
                     result = held([P, tiles, width], F32, "result%d_%d" % (c0, mt0))
-                    copy = nc.vector.tensor_copy if c1 == U and mt0 % 2 == 0 else nc.scalar.copy
+                    copy = nc.vector.tensor_copy if c1 == U else nc.scalar.copy
                     copy(out=result[:].rearrange("p a w -> p (a w)"), in_=acc[:, 0 : tiles * width])
                     nc.sync.dma_start(out_rows[:, mt0 : mt0 + tiles, c0:c1], result[:])

@@ -158,7 +158,7 @@ def tile_picked_blkmix_relu_p_kernel(
         stage(1)
         scatter(0, 0, H, values)
 
-        w1_grouped = held([P, N, PACK], BF16, "w1_grouped")
+        w1_grouped = held([P, N, PACK], BF16, "w1_grouped", "wa_grouped1")
         w1_scales = held([P, N], U8, "w1_scales")
         for m0 in range(0, N, P):
             interleave(gpsimd_copy, w1_grouped[:, m0 : m0 + P, :], w1_raw[:, :, m0 : m0 + P])
@@ -217,6 +217,6 @@ def tile_picked_blkmix_relu_p_kernel(
                             z_scales[:, c0:c1],
                         )
                     result = held([P, tiles, width], F32, "result%d_%d" % (c0, mt0))
-                    copy = nc.vector.tensor_copy if c1 == U else nc.scalar.copy
+                    copy = nc.vector.tensor_copy if c0 >= U // 2 and mt0 == 0 else nc.scalar.copy
                     copy(out=result[:].rearrange("p a w -> p (a w)"), in_=acc[:, 0 : tiles * width])
                     nc.sync.dma_start(out_rows[:, mt0 : mt0 + tiles, c0:c1], result[:])

@@ -25,7 +25,6 @@ LIST_ROWS = 16
 BANK = 512
 PIECES = ((0, 128), (128, 256), (256, 512))
 LAST_CUT = 384
-WARM_UPS = 2
 PARTS = ((0, 256), (256, 512), (512, 768), (768, 1024))
 HELPED = 1
 STEPS = ((0, 0, 128), (0, 128, 256), (1, 256, 512), (2, 512, 768), (3, 768, 1024))
@@ -182,9 +181,6 @@ def tile_picked_blkmix_relu_p_kernel(
         stage(3)
         scatter(2, 0, LAST_CUT, values)
         w1_codes = quantize_w1(0, 2 * P, "z3")
-        for i in range(WARM_UPS):
-            unread = psum.tile([P, BANK], F32, name="acc")
-            product(unread[:], w1_codes[i], w1_scales[:, i * P : (i + 1) * P], wa_codes[:], wa_scales[:])
         write_pair(gpsimd_copy, 0, HELPED, *PARTS[HELPED])
         for k in (0, 2):
             write_pair(nc.scalar.copy, 0, k, *PARTS[k])

@@ -16,6 +16,7 @@ RELU = mybir.ActivationFunctionType.Relu
 COPY = mybir.ActivationFunctionType.Copy
 MULT = mybir.AluOpType.mult
 ADD = mybir.AluOpType.add
+MAX = mybir.AluOpType.max
 
 P = 128
 PACK = 4
@@ -24,10 +25,8 @@ BLOCKS = S // (PACK * RUN)
 LIST_ROWS = 16
 BANK = 512
 PIECES = ((0, 128), (128, 256), (256, 512))
-LAST_CUT = 384
-PARTS = ((0, 256), (256, 512), (512, 768), (768, 1024))
-HELPED = 1
-STEPS = ((0, 0, 128), (0, 128, 256), (1, 256, 512), (2, 512, 768), (3, 768, 1024))
+HELPED = ((128, 256), (256, 512))
+STEPS = ((0, 128), (128, 256), (256, 512), (512, 768), (768, 1024))
 STORES = ((0, 128, 1), (128, 256, 2), (256, 512, 1), (512, 768, 2), (768, 1024, 2))
 
 
@@ -94,9 +93,10 @@ def tile_picked_blkmix_relu_p_kernel(
             nc.sync.dma_start(wa_raw[i][:], wa_rows[:, :, h0:h1])
             if i == 1:
                 nc.sync.dma_start(places[:], fl)
+        nc.sync.dma_start(gate[0][:], gt_rows[0])
         for t in range(PACK):
             nc.sync.dma_start(w1_raw[:, t, :], w1_rows[t])
-        for t in range(PACK):
+        for t in (1, 3, 2):
             nc.sync.dma_start(gate[t][:], gt_rows[t])
 
         z = [held([P, U if t % 2 else 2 * U], F32, "z%d" % t) for t in range(PACK)]
@@ -108,17 +108,20 @@ def tile_picked_blkmix_relu_p_kernel(
         wa_codes = held([P, H], U32, "wa_codes")
         wa_scales = held([P, H], U8, "wa_scales")
 
-        def prepare_wa(i):
+        def round_wa(i, copies):
             h0, h1 = PIECES[i]
-            grouped = held([P, h1 - h0, PACK], BF16, "wa_grouped%d" % i, "wa_grouped%d" % min(i, 1))
-            interleave(nc.scalar.copy, grouped[:], wa_raw[i][:])
-            quantize(wa_codes[:, h0:h1], wa_scales[:, h0:h1], grouped[:])
+            grouped = held([P, h1 - h0, PACK], BF16, "wa_grouped%d" % i)
+            width = (h1 - h0) // len(copies)
+            for n, copy in enumerate(copies):
+                cols = slice(n * width, (n + 1) * width)
+                interleave(copy, grouped[:, cols, :], wa_raw[i][:, :, cols])
+            return wa_codes[:, h0:h1], wa_scales[:, h0:h1], grouped[:]
 
         picked_scales = held([P, S], U8, "picked_scales")
         x_scale_plane = held([P, S], U8, "x_scale_plane")
         x_codes = held([P, S], U32, "x_codes")
         nc.vector.tensor_copy(picked_scales[:], table_scales[:].indirect(picks[:]))
-        prepare_wa(0)
+        quantize(*round_wa(0, [nc.scalar.copy]))
         nc.vector.tensor_copy(
             x_scale_plane[:].bitcast(I32).rearrange("p (t b w) -> p t b w", t=PACK, b=BLOCKS),
             picked_scales[:].bitcast(I32).rearrange("p (b t w) -> p t b w", t=PACK, b=BLOCKS),
@@ -128,75 +131,81 @@ def tile_picked_blkmix_relu_p_kernel(
             table_words[:].bitcast(U32).indirect(picks[:]),
         )
 
-        def project(t, h0, h1, offset):
+        def project(t, h0, h1):
             acc = psum.tile([P, BANK], F32, name="acc")
             cols = slice(t * P, (t + 1) * P)
             product(acc[:, 0 : h1 - h0], x_codes[:, cols], x_scale_plane[:, cols], wa_codes[:, h0:h1], wa_scales[:, h0:h1])
-            active = shared.tile([P, h1 - h0], F32, name="active%d_%d" % (t, h0), align_bytes=256, offset=offset)
-            nc.scalar.activation(out=active[:], in_=acc[:, 0 : h1 - h0], func=RELU)
-            return active
+            return acc[:, 0 : h1 - h0]
 
-        def weigh(t, active, name):
-            values = held(list(active.shape), F32, name)
-            nc.scalar.activation(out=values[:], in_=active, func=COPY, scale=gate[t][:])
-            return values
+        def window(t, h0, h1):
+            return z[t][:].indirect(places[:, h0 // LIST_ROWS : h1 // LIST_ROWS])
 
-        def scatter(t, h0, h1, values):
-            nc.vector.tensor_copy(z[t][:].indirect(places[:, h0 // LIST_ROWS : h1 // LIST_ROWS]), values[:])
+        quantize(*round_wa(1, [nc.scalar.copy]))
+        last_piece = round_wa(2, [nc.vector.tensor_copy, nc.scalar.copy])
 
-        def stage(t):
-            nc.scalar.activation(out=z[t - 1][:, U : 2 * U], in_=z[t][:], func=COPY, scale=gate[t][:])
-
-        prepare_wa(1)
-        for i, (h0, h1) in enumerate(PIECES):
-            if i == 1:
-                prepare_wa(2)
-            for n, t in enumerate((1, 3)):
-                scatter(t, h0, h1, project(t, h0, h1, 16 * h1 + 4 * n * (h1 - h0)))
-        values = weigh(0, project(0, 0, H, 20 * H)[:], "values0")
-        stage(1)
-        scatter(0, 0, H, values)
-
-        w1_grouped = held([P, N, PACK], BF16, "w1_grouped", "wa_grouped1")
         w1_scales = held([P, N], U8, "w1_scales")
+        w1_grouped = [held([P, N // 2, PACK], BF16, "w1_grouped%d" % half) for half in range(2)]
         for m0 in range(0, N, P):
-            interleave(gpsimd_copy, w1_grouped[:, m0 : m0 + P, :], w1_raw[:, :, m0 : m0 + P])
+            half, m = divmod(m0, N // 2)
+            interleave(gpsimd_copy, w1_grouped[half][:, m : m + P, :], w1_raw[:, :, m0 : m0 + P])
 
-        def quantize_w1(m0, m1, tag):
-            codes = held([P, m1 - m0], U32, "w1_codes%d" % m0, tag)
-            quantize(codes[:], w1_scales[:, m0:m1], w1_grouped[:, m0:m1, :])
-            return [codes[:, m : m + P] for m in range(0, m1 - m0, P)]
+        def quantize_w1(half, tag):
+            codes = held([P, N // 2], U32, "w1_codes%d" % half, tag)
+            quantize(codes[:], w1_scales[:, half * N // 2 : (half + 1) * N // 2], w1_grouped[half][:])
+            return [codes[:, 0:P], codes[:, P : 2 * P]]
 
-        z_grouped = [held([P, c1 - c0, PACK], BF16, "z_grouped%d" % k) for k, (c0, c1) in enumerate(PARTS)]
+        def activate(t, h0, h1, tag=None, offset=None):
+            acc = project(t, h0, h1)
+            name = "values%d_%d" % (t, h0)
+            if offset is None:
+                values = held([P, h1 - h0], F32, name, tag)
+            else:
+                values = shared.tile([P, h1 - h0], F32, name=name, align_bytes=256, offset=offset)
+            if t == 0:
+                nc.vector.tensor_scalar(values[:], acc, 0.0, gate[0][:], MAX, MULT)
+            elif t == 1:
+                nc.vector.tensor_scalar_max(values[:], acc, 0.0)
+            else:
+                nc.scalar.activation(out=values[:], in_=acc, func=RELU)
+            return values[:]
 
-        def write_pair(copy, t, k, c0, c1):
+        half = H // 2
+        first1, first3 = activate(1, 0, half, offset=16 * half), activate(3, 0, half, offset=20 * half)
+        quantize(*last_piece)
+        nc.vector.tensor_copy(window(1, 0, half), first1)
+        nc.scalar.activation(out=window(3, 0, half), in_=first3, func=COPY)
+        rest1, values0 = activate(1, half, H), activate(0, 0, H)
+        rest3, values2 = activate(3, half, H), activate(2, 0, H, "z_grouped")
+        nc.vector.tensor_copy(window(1, half, H), rest1)
+        nc.scalar.activation(out=window(3, half, H), in_=rest3, func=COPY)
+        nc.vector.tensor_scalar_mul(z[0][:, U : 2 * U], z[1][:], gate[1][:])
+        nc.scalar.activation(out=z[2][:, U : 2 * U], in_=z[3][:], func=COPY, scale=gate[3][:])
+        w1_codes = quantize_w1(0, "values1_%d" % half)
+        nc.vector.tensor_copy(window(0, 0, H), values0)
+        nc.scalar.activation(out=window(2, 0, H), in_=values2, func=COPY, scale=gate[2][:])
+
+        z_grouped = held([P, U, PACK], BF16, "z_grouped")
+
+        def write_pair(copy, t, c0, c1):
             interleave(
                 copy,
-                z_grouped[k][:, c0 - PARTS[k][0] : c1 - PARTS[k][0], t : t + 2],
+                z_grouped[:, c0:c1, t : t + 2],
                 z[t][:].rearrange("p (r w) -> p r w", r=2)[:, :, c0:c1],
             )
 
-        active = project(2, 0, H, 24 * H)
-        values = weigh(2, active[:, 0:LAST_CUT], "values2_first")
-        stage(3)
-        scatter(2, 0, LAST_CUT, values)
-        w1_codes = quantize_w1(0, 2 * P, "z3")
-        write_pair(gpsimd_copy, 0, HELPED, *PARTS[HELPED])
-        for k in (0, 2):
-            write_pair(nc.scalar.copy, 0, k, *PARTS[k])
-        scatter(2, LAST_CUT, H, weigh(2, active[:, LAST_CUT:H], "values2_last"))
-        write_pair(nc.scalar.copy, 0, 3, *PARTS[3])
-        write_pair(nc.scalar.copy, 2, HELPED, *PARTS[HELPED])
+        for c0, c1 in HELPED:
+            write_pair(nc.scalar.copy, 2, c0, c1)
 
         out_rows = out.rearrange("(mt p) w -> p mt w", p=P)
         z_codes = held([P, U], U32, "z_codes")
         z_scales = held([P, U], U8, "z_scales")
-        for k, q0, q1 in STEPS:
-            if k != HELPED:
-                write_pair(nc.vector.tensor_copy, 2, k, q0, q1)
+        for q0, q1 in STEPS:
+            write_pair(nc.vector.tensor_copy, 0, q0, q1)
+            if (q0, q1) not in HELPED:
+                write_pair(nc.vector.tensor_copy, 2, q0, q1)
             if q0 == 0:
-                w1_codes += quantize_w1(2 * P, N, "values2_last")
-            quantize(z_codes[:, q0:q1], z_scales[:, q0:q1], z_grouped[k][:, q0 - PARTS[k][0] : q1 - PARTS[k][0], :])
+                w1_codes += quantize_w1(1, "values0_0")
+            quantize(z_codes[:, q0:q1], z_scales[:, q0:q1], z_grouped[:, q0:q1, :])
             for c0, c1, tiles in STORES:
                 if c1 != q1:
                     continue

@@ -25,8 +25,9 @@ BLOCKS = S // (PACK * RUN)
 LIST_ROWS = 16
 BANK = 512
 PIECES = ((0, 128), (128, 256), (256, 512))
-HELPED = ((128, 256), (256, 512))
-STEPS = ((0, 128), (128, 256), (256, 512), (512, 768), (768, 1024))
+PARTS = ((0, 128), (128, 512), (512, 1024))
+HELPED = 256
+STEPS = ((0, 0, 128), (1, 128, 256), (1, 256, 512), (2, 512, 768), (2, 768, 1024))
 STORES = ((0, 128, 1), (128, 256, 2), (256, 512, 1), (512, 768, 2), (768, 1024, 2))
 
 
@@ -93,17 +94,15 @@ def tile_picked_blkmix_relu_p_kernel(
             nc.sync.dma_start(wa_raw[i][:], wa_rows[:, :, h0:h1])
             if i == 1:
                 nc.sync.dma_start(places[:], fl)
-        nc.sync.dma_start(gate[0][:], gt_rows[0])
+                for t in range(PACK):
+                    nc.sync.dma_start(gate[t][:], gt_rows[t])
         for t in range(PACK):
             nc.sync.dma_start(w1_raw[:, t, :], w1_rows[t])
-        for t in (1, 3, 2):
-            nc.sync.dma_start(gate[t][:], gt_rows[t])
 
-        z = [held([P, U if t % 2 else 2 * U], F32, "z%d" % t) for t in range(PACK)]
-        for t in (1, 3):
+        z = [held([P, U], F32, "z%d" % t) for t in range(PACK)]
+        for t in (0, 1):
             nc.vector.memset(z[t][:], 0.0)
-        for t in (0, 2):
-            nc.scalar.activation(out=z[t][:, 0:U], in_=z[t + 1][:], func=COPY)
+            nc.scalar.activation(out=z[t + 2][:], in_=z[t][:], func=COPY)
 
         wa_codes = held([P, H], U32, "wa_codes")
         wa_scales = held([P, H], U8, "wa_scales")
@@ -147,65 +146,68 @@ def tile_picked_blkmix_relu_p_kernel(
         w1_grouped = [held([P, N // 2, PACK], BF16, "w1_grouped%d" % half) for half in range(2)]
         for m0 in range(0, N, P):
             half, m = divmod(m0, N // 2)
-            interleave(gpsimd_copy, w1_grouped[half][:, m : m + P, :], w1_raw[:, :, m0 : m0 + P])
+            gpsimd_copy(w1_grouped[half][:, m : m + P, :], w1_raw[:, :, m0 : m0 + P].rearrange("p t m -> p m t"))
 
         def quantize_w1(half, tag):
             codes = held([P, N // 2], U32, "w1_codes%d" % half, tag)
             quantize(codes[:], w1_scales[:, half * N // 2 : (half + 1) * N // 2], w1_grouped[half][:])
             return [codes[:, 0:P], codes[:, P : 2 * P]]
 
-        def activate(t, h0, h1, tag=None, offset=None):
+        def activate(t, h0, h1, offset=None):
             acc = project(t, h0, h1)
             name = "values%d_%d" % (t, h0)
             if offset is None:
-                values = held([P, h1 - h0], F32, name, tag)
+                values = held([P, h1 - h0], F32, name)
             else:
                 values = shared.tile([P, h1 - h0], F32, name=name, align_bytes=256, offset=offset)
-            if t == 0:
-                nc.vector.tensor_scalar(values[:], acc, 0.0, gate[0][:], MAX, MULT)
-            elif t == 1:
-                nc.vector.tensor_scalar_max(values[:], acc, 0.0)
+            if t % 2 == 0:
+                nc.vector.tensor_scalar(values[:], acc, 0.0, gate[t][:], MAX, MULT)
             else:
                 nc.scalar.activation(out=values[:], in_=acc, func=RELU)
             return values[:]
 
+        def scatter(t, h0, h1, values):
+            if t % 2 == 0:
+                nc.vector.tensor_copy(window(t, h0, h1), values)
+            else:
+                nc.scalar.activation(out=window(t, h0, h1), in_=values, func=COPY, scale=gate[t][:])
+
         half = H // 2
-        first1, first3 = activate(1, 0, half, offset=16 * half), activate(3, 0, half, offset=20 * half)
+        first = [activate(t, 0, half, 16 * half + 4 * half * t) for t in (0, 1)]
         quantize(*last_piece)
-        nc.vector.tensor_copy(window(1, 0, half), first1)
-        nc.scalar.activation(out=window(3, 0, half), in_=first3, func=COPY)
-        rest1, values0 = activate(1, half, H), activate(0, 0, H)
-        rest3, values2 = activate(3, half, H), activate(2, 0, H, "z_grouped")
-        nc.vector.tensor_copy(window(1, half, H), rest1)
-        nc.scalar.activation(out=window(3, half, H), in_=rest3, func=COPY)
-        nc.vector.tensor_scalar_mul(z[0][:, U : 2 * U], z[1][:], gate[1][:])
-        nc.scalar.activation(out=z[2][:, U : 2 * U], in_=z[3][:], func=COPY, scale=gate[3][:])
-        w1_codes = quantize_w1(0, "values1_%d" % half)
-        nc.vector.tensor_copy(window(0, 0, H), values0)
-        nc.scalar.activation(out=window(2, 0, H), in_=values2, func=COPY, scale=gate[2][:])
+        for t in (0, 1):
+            scatter(t, 0, half, first[t])
+        rest = [(activate(t, half, H), activate(t + 2, 0, H)) for t in (0, 1)]
+        for t in (0, 1):
+            scatter(t, half, H, rest[t][0])
+            scatter(t + 2, 0, H, rest[t][1])
 
-        z_grouped = held([P, U, PACK], BF16, "z_grouped")
-
-        def write_pair(copy, t, c0, c1):
-            interleave(
-                copy,
-                z_grouped[:, c0:c1, t : t + 2],
-                z[t][:].rearrange("p (r w) -> p r w", r=2)[:, :, c0:c1],
-            )
-
-        for c0, c1 in HELPED:
-            write_pair(nc.scalar.copy, 2, c0, c1)
+        planes = [
+            held([P, PACK, c1 - c0], F32, "planes%d" % c0, "values1_%d" % half if c1 == U else None) for c0, c1 in PARTS
+        ]
+        for part, (c0, c1) in zip(planes, PARTS):
+            for t in (0, 1):
+                nc.sync.dma_start(part[:, t, :], z[t][:, c0:c1])
+        for part, (c0, c1), copy in zip(planes, PARTS, (nc.vector.tensor_copy, nc.scalar.copy, nc.sync.dma_start)):
+            for t in (2, 3):
+                copy(part[:, t, :], z[t][:, c0:c1])
+        head = STEPS[0][2]
+        z_head = held([P, head, PACK], BF16, "z_head", "z_grouped")
+        z_rest = held([P, U - head, PACK], BF16, "z_rest", "z_grouped")
 
         out_rows = out.rearrange("(mt p) w -> p mt w", p=P)
         z_codes = held([P, U], U32, "z_codes")
         z_scales = held([P, U], U8, "z_scales")
-        for q0, q1 in STEPS:
-            write_pair(nc.vector.tensor_copy, 0, q0, q1)
-            if (q0, q1) not in HELPED:
-                write_pair(nc.vector.tensor_copy, 2, q0, q1)
+        for k, q0, q1 in STEPS:
+            grouped = z_rest[:, q0 - head : q1 - head, :] if q0 else z_head[:]
+            if q0 == HELPED:
+                grouped = held([P, q1 - q0, PACK], BF16, "z_helped")[:]
             if q0 == 0:
-                w1_codes += quantize_w1(1, "values0_0")
-            quantize(z_codes[:, q0:q1], z_scales[:, q0:q1], z_grouped[:, q0:q1, :])
+                w1_codes = quantize_w1(0, "values2_0")
+            interleave(nc.scalar.copy if q0 == HELPED else nc.vector.tensor_copy, grouped, planes[k][:, :, q0 - PARTS[k][0] : q1 - PARTS[k][0]])
+            quantize(z_codes[:, q0:q1], z_scales[:, q0:q1], grouped)
+            if q0 == 0:
+                w1_codes += quantize_w1(1, "planes0")
             for c0, c1, tiles in STORES:
                 if c1 != q1:
                     continue

@@ -24,11 +24,13 @@ RUN = 8
 BLOCKS = S // (PACK * RUN)
 LIST_ROWS = 16
 BANK = 512
-PIECES = ((0, 128), (128, 256), (256, 512))
+PIECES = ((0, 256), (256, 512))
+VECTOR_SHARE = 96
 PARTS = ((0, 128), (128, 512), (512, 1024))
-HELPED = 256
-STEPS = ((0, 0, 128), (1, 128, 256), (1, 256, 512), (2, 512, 768), (2, 768, 1024))
-STORES = ((0, 128, 1), (128, 256, 2), (256, 512, 1), (512, 768, 2), (768, 1024, 2))
+HELPED = (256, 384)
+LAST = 768
+STEPS = ((0, 0, 128), (1, 128, 256), (1, 256, 512), (2, 512, 768), (2, 768, 896), (2, 896, 1024))
+STORES = ((0, 128, 2), (128, 256, 2), (256, 512, 1), (512, 768, 2), (768, 1024, 2))
 
 
 def interleave(copy, grouped, raw):
@@ -90,12 +92,11 @@ def tile_picked_blkmix_relu_p_kernel(
         for r in range(4):
             nc.sync.dma_start(table_scales[r:P:32, :].bitcast(I32), x_scales[0, r:16:4, :].bitcast(I32))
         nc.sync.dma_start(table_words[:], words)
-        for i, (h0, h1) in list(enumerate(PIECES))[1:]:
-            nc.sync.dma_start(wa_raw[i][:], wa_rows[:, :, h0:h1])
-            if i == 1:
-                nc.sync.dma_start(places[:], fl)
-                for t in range(PACK):
-                    nc.sync.dma_start(gate[t][:], gt_rows[t])
+        nc.sync.dma_start(wa_raw[1][:], wa_rows[:, :, PIECES[1][0] : H])
+        nc.sync.dma_start(gate[0][:], gt_rows[0])
+        nc.sync.dma_start(places[:], fl)
+        for t in range(1, PACK):
+            nc.sync.dma_start(gate[t][:], gt_rows[t])
         for t in range(PACK):
             nc.sync.dma_start(w1_raw[:, t, :], w1_rows[t])
 
@@ -107,20 +108,19 @@ def tile_picked_blkmix_relu_p_kernel(
         wa_codes = held([P, H], U32, "wa_codes")
         wa_scales = held([P, H], U8, "wa_scales")
 
-        def round_wa(i, copies):
+        def round_wa(i, on_vector):
             h0, h1 = PIECES[i]
             grouped = held([P, h1 - h0, PACK], BF16, "wa_grouped%d" % i)
-            width = (h1 - h0) // len(copies)
-            for n, copy in enumerate(copies):
-                cols = slice(n * width, (n + 1) * width)
-                interleave(copy, grouped[:, cols, :], wa_raw[i][:, :, cols])
+            if on_vector:
+                interleave(nc.vector.tensor_copy, grouped[:, 0:on_vector, :], wa_raw[i][:, :, 0:on_vector])
+            interleave(nc.scalar.copy, grouped[:, on_vector:, :], wa_raw[i][:, :, on_vector:])
             return wa_codes[:, h0:h1], wa_scales[:, h0:h1], grouped[:]
 
         picked_scales = held([P, S], U8, "picked_scales")
         x_scale_plane = held([P, S], U8, "x_scale_plane")
         x_codes = held([P, S], U32, "x_codes")
         nc.vector.tensor_copy(picked_scales[:], table_scales[:].indirect(picks[:]))
-        quantize(*round_wa(0, [nc.scalar.copy]))
+        quantize(*round_wa(0, 0))
         nc.vector.tensor_copy(
             x_scale_plane[:].bitcast(I32).rearrange("p (t b w) -> p t b w", t=PACK, b=BLOCKS),
             picked_scales[:].bitcast(I32).rearrange("p (b t w) -> p t b w", t=PACK, b=BLOCKS),
@@ -139,8 +139,7 @@ def tile_picked_blkmix_relu_p_kernel(
         def window(t, h0, h1):
             return z[t][:].indirect(places[:, h0 // LIST_ROWS : h1 // LIST_ROWS])
 
-        quantize(*round_wa(1, [nc.scalar.copy]))
-        last_piece = round_wa(2, [nc.vector.tensor_copy, nc.scalar.copy])
+        last_piece = round_wa(1, VECTOR_SHARE)
 
         w1_scales = held([P, N], U8, "w1_scales")
         w1_grouped = [held([P, N // 2, PACK], BF16, "w1_grouped%d" % half) for half in range(2)]
@@ -191,6 +190,12 @@ def tile_picked_blkmix_relu_p_kernel(
         for part, (c0, c1), copy in zip(planes, PARTS, (nc.vector.tensor_copy, nc.scalar.copy, nc.sync.dma_start)):
             for t in (2, 3):
                 copy(part[:, t, :], z[t][:, c0:c1])
+        z_helped = held([P, 256, PACK], BF16, "z_helped")
+        interleave(
+            nc.scalar.copy,
+            z_helped[:, 0 : HELPED[1] - HELPED[0], :],
+            planes[1][:, :, HELPED[0] - PARTS[1][0] : HELPED[1] - PARTS[1][0]],
+        )
         head = STEPS[0][2]
         z_head = held([P, head, PACK], BF16, "z_head", "z_grouped")
         z_rest = held([P, U - head, PACK], BF16, "z_rest", "z_grouped")
@@ -199,12 +204,16 @@ def tile_picked_blkmix_relu_p_kernel(
         z_codes = held([P, U], U32, "z_codes")
         z_scales = held([P, U], U8, "z_scales")
         for k, q0, q1 in STEPS:
-            grouped = z_rest[:, q0 - head : q1 - head, :] if q0 else z_head[:]
-            if q0 == HELPED:
-                grouped = held([P, q1 - q0, PACK], BF16, "z_helped")[:]
+            raw = planes[k][:, :, q0 - PARTS[k][0] : q1 - PARTS[k][0]]
             if q0 == 0:
+                grouped = z_head[:]
                 w1_codes = quantize_w1(0, "values2_0")
-            interleave(nc.scalar.copy if q0 == HELPED else nc.vector.tensor_copy, grouped, planes[k][:, :, q0 - PARTS[k][0] : q1 - PARTS[k][0]])
+            elif q0 == HELPED[0]:
+                grouped = z_helped[:]
+            else:
+                grouped = z_rest[:, q0 - head : q1 - head, :]
+            first_own = HELPED[1] - q0 if q0 == HELPED[0] else 0
+            interleave(nc.vector.tensor_copy, grouped[:, first_own:, :], raw[:, :, first_own:])
             quantize(z_codes[:, q0:q1], z_scales[:, q0:q1], grouped)
             if q0 == 0:
                 w1_codes += quantize_w1(1, "planes0")
@@ -224,6 +233,6 @@ def tile_picked_blkmix_relu_p_kernel(
                             z_scales[:, c0:c1],
                         )
                     result = held([P, tiles, width], F32, "result%d_%d" % (c0, mt0))
-                    copy = nc.vector.tensor_copy if c0 >= U // 2 and mt0 == 0 else nc.scalar.copy
+                    copy = nc.vector.tensor_copy if c0 >= LAST and mt0 == 0 else nc.scalar.copy
                     copy(out=result[:].rearrange("p a w -> p (a w)"), in_=acc[:, 0 : tiles * width])
                     nc.sync.dma_start(out_rows[:, mt0 : mt0 + tiles, c0:c1], result[:])

from contextlib import ExitStack

import concourse.mybir as mybir

K, T, S, N, U, H = 512, 2048, 512, 512, 1024, 512
FLOPS = 2 * K * S * H + 2 * S * N * U

F32 = mybir.dt.float32
BF16 = mybir.dt.bfloat16
I32 = mybir.dt.int32
U32 = mybir.dt.uint32
U16 = mybir.dt.uint16
U8 = mybir.dt.uint8
FP8X4 = mybir.dt.float8_e4m3fn_x4
RELU = mybir.ActivationFunctionType.Relu
COPY = mybir.ActivationFunctionType.Copy
MULT = mybir.AluOpType.mult
ADD = mybir.AluOpType.add
MAX = mybir.AluOpType.max

P = 128
PACK = 4
RUN = 8
BLOCKS = S // (PACK * RUN)
LIST_ROWS = 16
BANK = 512
PIECES = ((0, 256), (256, 512))
VECTOR_SHARE = 96
PARTS = ((0, 128), (128, 512), (512, 1024))
HELPED = (256, 384)
LAST = 768
STEPS = ((0, 0, 128), (1, 128, 256), (1, 256, 512), (2, 512, 768), (2, 768, 896), (2, 896, 1024))
STORES = ((0, 128, 2), (128, 256, 2), (256, 512, 1), (512, 768, 2), (768, 1024, 2))


def interleave(copy, grouped, raw):
    copy(
        out=grouped.rearrange("p (c i) t -> p c t i", i=4),
        in_=raw.rearrange("p t (c i) -> p c t i", i=4),
    )


def tile_picked_blkmix_relu_p_kernel(
    tc, x_words, x_scales, wa, gt, w1, offs, fl, out
):
    nc = tc.nc
    with ExitStack() as ctx:
        keep = ctx.enter_context(tc.tile_pool(name="keep", bufs=1))
        shared = ctx.enter_context(tc.tile_pool(name="shared", bufs=1))
        psum = ctx.enter_context(tc.psum_pool(name="psum", bufs=8))

        def held(shape, dtype, name, tag=None):
            return keep.tile(shape, dtype, name=name, tag=tag or name, align_bytes=256)

        def quantize(codes, scales, grouped):
            nc.vector.quantize_mx(
                out=codes.bitcast(FP8X4), scales=scales, in_=grouped.rearrange("p w j -> p (w j)")
            )

        def product(acc, lhs, lhs_scale, rhs, rhs_scale):
            nc.tensor.matmul_mx(
                out=acc,
                lhsT=lhs.bitcast(FP8X4),
                lhsT_scale=lhs_scale,
                rhs=rhs.bitcast(FP8X4),
                rhs_scale=rhs_scale,
                start=True,
                stop=True,
            )

        def gpsimd_copy(out, in_):
            nc.gpsimd.tensor_scalar(out, in_, 1.0, 0.0, MULT, ADD)

        picks = keep.tile([P, S // LIST_ROWS], U16, name="picks")
        places = keep.tile([P, H // LIST_ROWS], U16, name="places")
        table_words = held([P, T], I32, "table_words")
        table_scales = held([P, T], U8, "table_scales")
        gate = [keep.tile([P, 1], F32, name="gate%d" % t) for t in range(PACK)]
        wa_raw = [
            shared.tile([P, PACK, h1 - h0], F32, name="wa_raw%d" % i, align_bytes=256, offset=16 * h0)
            for i, (h0, h1) in enumerate(PIECES)
        ]
        w1_raw = held([P, PACK, N], F32, "w1_raw")

        nc.vector.memset(table_scales[:].bitcast(I32), 0)
        words = x_words[0].rearrange("p n t -> p (n t)").bitcast(I32)
        wa_rows = wa.rearrange("(p j) h -> p j h", j=PACK)
        gt_rows = gt.rearrange("(b t q) o -> t b q o", t=PACK, q=RUN)
        w1_rows = w1.rearrange("(b t q) m -> t b q m", t=PACK, q=RUN)
        nc.sync.dma_start(wa_raw[0][:], wa_rows[:, :, 0 : PIECES[0][1]])
        nc.sync.dma_start(picks[:], offs)
        for r in range(4):
            nc.sync.dma_start(table_scales[r:P:32, :].bitcast(I32), x_scales[0, r:16:4, :].bitcast(I32))
        nc.sync.dma_start(table_words[:], words)
        nc.sync.dma_start(wa_raw[1][:], wa_rows[:, :, PIECES[1][0] : H])
        nc.sync.dma_start(gate[0][:], gt_rows[0])
        nc.sync.dma_start(places[:], fl)
        for t in range(1, PACK):
            nc.sync.dma_start(gate[t][:], gt_rows[t])
        for t in range(PACK):
            nc.sync.dma_start(w1_raw[:, t, :], w1_rows[t])

        z = [held([P, U], F32, "z%d" % t) for t in range(PACK)]
        for t in (0, 1):
            nc.vector.memset(z[t][:], 0.0)
            nc.scalar.activation(out=z[t + 2][:], in_=z[t][:], func=COPY)

        wa_codes = held([P, H], U32, "wa_codes")
        wa_scales = held([P, H], U8, "wa_scales")

        def round_wa(i, on_vector):
            h0, h1 = PIECES[i]
            grouped = held([P, h1 - h0, PACK], BF16, "wa_grouped%d" % i)
            if on_vector:
                interleave(nc.vector.tensor_copy, grouped[:, 0:on_vector, :], wa_raw[i][:, :, 0:on_vector])
            interleave(nc.scalar.copy, grouped[:, on_vector:, :], wa_raw[i][:, :, on_vector:])
            return wa_codes[:, h0:h1], wa_scales[:, h0:h1], grouped[:]

        picked_scales = held([P, S], U8, "picked_scales")
        x_scale_plane = held([P, S], U8, "x_scale_plane")
        x_codes = held([P, S], U32, "x_codes")
        nc.vector.tensor_copy(picked_scales[:], table_scales[:].indirect(picks[:]))
        quantize(*round_wa(0, 0))
        nc.vector.tensor_copy(
            x_scale_plane[:].bitcast(I32).rearrange("p (t b w) -> p t b w", t=PACK, b=BLOCKS),
            picked_scales[:].bitcast(I32).rearrange("p (b t w) -> p t b w", t=PACK, b=BLOCKS),
        )
        nc.vector.tensor_copy(
            x_codes[:].rearrange("p (t b q) -> p b t q", t=PACK, q=RUN),
            table_words[:].bitcast(U32).indirect(picks[:]),
        )

        def project(t, h0, h1):
            acc = psum.tile([P, BANK], F32, name="acc")
            cols = slice(t * P, (t + 1) * P)
            product(acc[:, 0 : h1 - h0], x_codes[:, cols], x_scale_plane[:, cols], wa_codes[:, h0:h1], wa_scales[:, h0:h1])
            return acc[:, 0 : h1 - h0]

        def window(t, h0, h1):
            return z[t][:].indirect(places[:, h0 // LIST_ROWS : h1 // LIST_ROWS])

        last_piece = round_wa(1, VECTOR_SHARE)

        w1_scales = held([P, N], U8, "w1_scales")
        w1_grouped = [held([P, N // 2, PACK], BF16, "w1_grouped%d" % half) for half in range(2)]
        for m0 in range(0, N, P):
            half, m = divmod(m0, N // 2)
            gpsimd_copy(w1_grouped[half][:, m : m + P, :], w1_raw[:, :, m0 : m0 + P].rearrange("p t m -> p m t"))

        def quantize_w1(half, tag):
            codes = held([P, N // 2], U32, "w1_codes%d" % half, tag)
            quantize(codes[:], w1_scales[:, half * N // 2 : (half + 1) * N // 2], w1_grouped[half][:])
            return [codes[:, 0:P], codes[:, P : 2 * P]]

        def activate(t, h0, h1, offset=None):
            acc = project(t, h0, h1)
            name = "values%d_%d" % (t, h0)
            if offset is None:
                values = held([P, h1 - h0], F32, name)
            else:
                values = shared.tile([P, h1 - h0], F32, name=name, align_bytes=256, offset=offset)
            if t % 2 == 0:
                nc.vector.tensor_scalar(values[:], acc, 0.0, gate[t][:], MAX, MULT)
            else:
                nc.scalar.activation(out=values[:], in_=acc, func=RELU)
            return values[:]

        def scatter(t, h0, h1, values):
            if t % 2 == 0:
                nc.vector.tensor_copy(window(t, h0, h1), values)
            else:
                nc.scalar.activation(out=window(t, h0, h1), in_=values, func=COPY, scale=gate[t][:])

        half = H // 2
        first = [activate(t, 0, half, 16 * half + 4 * half * t) for t in (0, 1)]
        quantize(*last_piece)
        for t in (0, 1):
            scatter(t, 0, half, first[t])
        rest = [(activate(t, half, H), activate(t + 2, 0, H)) for t in (0, 1)]
        for t in (0, 1):
            scatter(t, half, H, rest[t][0])
            scatter(t + 2, 0, H, rest[t][1])

        planes = [
            held([P, PACK, c1 - c0], F32, "planes%d" % c0, "values1_%d" % half if c1 == U else None) for c0, c1 in PARTS
        ]
        for part, (c0, c1) in zip(planes, PARTS):
            for t in (0, 1):
                nc.sync.dma_start(part[:, t, :], z[t][:, c0:c1])
        for part, (c0, c1), copy in zip(planes, PARTS, (nc.vector.tensor_copy, nc.scalar.copy, nc.sync.dma_start)):
            for t in (2, 3):
                copy(part[:, t, :], z[t][:, c0:c1])
        z_helped = held([P, 256, PACK], BF16, "z_helped")
        interleave(
            nc.scalar.copy,
            z_helped[:, 0 : HELPED[1] - HELPED[0], :],
            planes[1][:, :, HELPED[0] - PARTS[1][0] : HELPED[1] - PARTS[1][0]],
        )
        head = STEPS[0][2]
        z_head = held([P, head, PACK], BF16, "z_head", "z_grouped")
        z_rest = held([P, U - head, PACK], BF16, "z_rest", "z_grouped")

        out_rows = out.rearrange("(mt p) w -> p mt w", p=P)
        z_codes = held([P, U], U32, "z_codes")
        z_scales = held([P, U], U8, "z_scales")
        for k, q0, q1 in STEPS:
            raw = planes[k][:, :, q0 - PARTS[k][0] : q1 - PARTS[k][0]]
            if q0 == 0:
                grouped = z_head[:]
                w1_codes = quantize_w1(0, "values2_0")
            elif q0 == HELPED[0]:
                grouped = z_helped[:]
            else:
                grouped = z_rest[:, q0 - head : q1 - head, :]
            first_own = HELPED[1] - q0 if q0 == HELPED[0] else 0
            interleave(nc.vector.tensor_copy, grouped[:, first_own:, :], raw[:, :, first_own:])
            quantize(z_codes[:, q0:q1], z_scales[:, q0:q1], grouped)
            if q0 == 0:
                w1_codes += quantize_w1(1, "planes0")
            for c0, c1, tiles in STORES:
                if c1 != q1:
                    continue
                width = c1 - c0
                for mt0 in range(0, N // P, tiles):
                    acc = psum.tile([P, BANK], F32, name="acc")
                    for i in range(tiles):
                        rows = slice((mt0 + i) * P, (mt0 + i + 1) * P)
                        product(
                            acc[:, i * width : (i + 1) * width],
                            w1_codes[mt0 + i],
                            w1_scales[:, rows],
                            z_codes[:, c0:c1],
                            z_scales[:, c0:c1],
                        )
                    result = held([P, tiles, width], F32, "result%d_%d" % (c0, mt0))
                    copy = nc.vector.tensor_copy if c0 >= LAST and mt0 == 0 else nc.scalar.copy
                    copy(out=result[:].rearrange("p a w -> p (a w)"), in_=acc[:, 0 : tiles * width])
                    nc.sync.dma_start(out_rows[:, mt0 : mt0 + tiles, c0:c1], result[:])
